import numpy as np
import ml_dtypes


def mxq(x, axis, fmt="e4m3"):
    dtype, down = {"e4m3": (ml_dtypes.float8_e4m3fn, 7), "e5m2": (ml_dtypes.float8_e5m2, 14)}[fmt]
    v = np.moveaxis(np.asarray(x, np.float32).astype(ml_dtypes.bfloat16).astype(np.float64), axis, -1)
    blocks = v.reshape(v.shape[:-1] + (-1, 32))
    amax = np.abs(blocks).max(-1, keepdims=True)
    byte = np.maximum(np.where(amax > 0, np.frexp(amax)[1] - 1 + 127, 0) - down, 1)
    scale = np.exp2(byte - 127.0)
    codes = (blocks / scale).astype(np.float32).astype(dtype).astype(np.float64)
    return np.moveaxis((codes * scale).reshape(v.shape), -1, axis)


WIDE = False


def mx_kscale(k):
    if not WIDE:
        return np.ones(k)
    levels = np.array([10, -10, 5, -5, 0])
    if k % 512:
        return np.exp2(np.random.permutation(np.resize(levels, k // 32))).repeat(32)
    a = np.empty((k // 512, 16))
    for p in range(k // 512):
        a[p, :8] = np.random.permutation(np.resize(levels, 8))
        for g in range(8):
            far = levels[np.abs(levels - a[p, g]) >= 10]
            a[p, g + 8] = far[np.random.randint(len(far))]
    return np.exp2(a.ravel()).repeat(32)


def f64(x):
    return np.asarray(x).astype(np.float64)


def striped(idx):
    return np.tile(idx.reshape(-1, 16).T, (8, 1)).astype(np.uint16)


def unstriped(offs):
    return offs[:16].T.reshape(-1).astype(np.int64)


E2M1 = np.array([0.0, 0.5, 1.0, 1.5, 2.0, 3.0, 4.0, 6.0, -0.0, -0.5, -1.0, -1.5, -2.0, -3.0, -4.0, -6.0])


def pack_weight(w, fmt):
    k, n = w.shape
    w = f64(np.asarray(w, np.float32).astype(ml_dtypes.bfloat16)).reshape(k // 32, 32, n)
    amax = np.abs(w).max(1)
    if fmt == "e4m3":
        byte = np.frexp(amax)[1] - 1 + 127 - 7
    else:
        mant, ex = np.frexp(amax / 6.0)
        byte = np.where(mant > 0.5, ex, ex - 1) + 127
    byte = np.clip(np.where(amax > 0, byte, 1), 1, 254)
    scaled = (w * np.exp2(127.0 - byte)[:, None, :]).reshape(k, n).astype(np.float32)
    by_word = np.ascontiguousarray(scaled.reshape(k // 512, 128, 4, n).transpose(0, 1, 3, 2))
    if fmt == "e4m3":
        words = by_word.astype(ml_dtypes.float8_e4m3fn).view(np.uint8)
    else:
        c = by_word.astype(ml_dtypes.float4_e2m1fn).view(np.uint8) & 0xF
        words = (c[..., 0::2] | (c[..., 1::2] << 4)).reshape(k // 512, 128, 2 * n)
    return np.ascontiguousarray(words), np.ascontiguousarray(byte.astype(np.uint8).reshape(k // 512, 16, n))


def unpack_weight(words, scales, fmt):
    g, _, n = scales.shape
    words = np.ascontiguousarray(words).reshape(g, 128, n, -1)
    if fmt == "e4m3":
        vals = words.view(ml_dtypes.float8_e4m3fn).astype(np.float64)
    else:
        nib = np.empty((g, 128, n, 4), np.uint8)
        nib[..., 0::2] = words & 0xF
        nib[..., 1::2] = words >> 4
        vals = E2M1[nib]
    vals = vals * np.repeat(np.exp2(scales.astype(np.float64) - 127.0), 8, axis=1)[..., None]
    return vals.transpose(0, 1, 3, 2).reshape(g * 512, n)


def gelu(v):
    return 0.5 * v * (1.0 + np.tanh(np.sqrt(2.0 / np.pi) * (v + 0.044715 * v**3)))


K, H, N, T, S = 1024, 512, 384, 2048, 1024

def setup_inputs():
    n = np.random.standard_normal
    s = mx_kscale(K)[:, None]
    u = mx_kscale(H)[:, None]
    frames = n((K, T)) * np.exp(0.4 * n(T)) * s
    tab_words, tab_scales = pack_weight(frames, "e4m3")
    phase = 2 * np.pi * np.arange(K)[:, None] * (np.arange(H) + 0.5)[None, :] / K
    wc = np.sqrt(2 / K) * np.cos(phase) / s * np.sqrt(u.T)
    ws = np.sqrt(2 / K) * np.sin(phase) / s * np.sqrt(u.T)
    wm_words, wm_scales = pack_weight(np.square(np.square(n((H, N)))) / (3 * H) / u, "e2m1")
    gT = 0.5 * np.abs(n((N, T)))
    offs = striped(np.random.permutation(T)[:S])
    return {"tab_words": tab_words, "tab_scales": tab_scales, "offs": offs,
            "wc": wc.astype(np.float32), "ws": ws.astype(np.float32),
            "wm_words": wm_words, "wm_scales": wm_scales, "gT": gT.astype(np.float32)}

def reference(tab_words, tab_scales, offs, wc, ws, wm_words, wm_scales, gT):
    v = unpack_weight(tab_words, tab_scales, "e4m3")[:, unstriped(offs)]
    g = f64(gT)[:, unstriped(offs)]
    c = mxq(f64(wc), 0, "e4m3").T @ v
    d = mxq(f64(ws), 0, "e4m3").T @ v
    pc = mxq(np.square(c), 0, "e4m3")
    ps = mxq(np.square(d), 0, "e4m3")
    wm = unpack_weight(wm_words, wm_scales, "e2m1")
    p = wm.T @ pc + wm.T @ ps
    return np.log(1.0 + p) - g

@@ -1,0 +1,231 @@
+from contextlib import ExitStack
+
+import concourse.mybir as mybir
+
+K, H, N, T, S = 1024, 512, 384, 2048, 1024
+FLOPS = 2 * (2 * K * H * S + 2 * H * N * S)
+
+F32 = mybir.dt.float32
+BF16 = mybir.dt.bfloat16
+I32 = mybir.dt.int32
+U32 = mybir.dt.uint32
+U16 = mybir.dt.uint16
+U8 = mybir.dt.uint8
+FP8X4 = mybir.dt.float8_e4m3fn_x4
+FP4X4 = mybir.dt.float4_e2m1fn_x4
+ACT = mybir.ActivationFunctionType
+ALU = mybir.AluOpType
+
+P = 128
+PASSES = 2
+BLK = 128
+NBLK = S // BLK
+SL = 256
+NSL = S // SL
+NT = N // P
+
+
+def tile_list_voiced_log_spectra_kernel(tc, tab_words, tab_scales, offs, wc, ws, wm_words, wm_scales, gT, out):
+    nc = tc.nc
+    with ExitStack() as ctx:
+        keep = ctx.enter_context(tc.tile_pool(name="keep", bufs=1))
+        psum = ctx.enter_context(tc.psum_pool(name="psum", bufs=8))
+
+        offsets = keep.tile([P, S // 16], U16, name="offsets")
+        tabw = [keep.tile([P, T], I32, name=f"tabw{a}", align_bytes=64) for a in range(PASSES)]
+        tabs = keep.tile([P, T // 4], I32, name="tabs", align_bytes=64)
+        vw = [keep.tile([P, S], U32, name=f"vw{a}", align_bytes=64) for a in range(PASSES)]
+        vs = keep.tile([P, S], U8, name="vs", align_bytes=64)
+        wraw = [[keep.tile([P, 4, H], F32, name=f"wraw{m}{a}", align_bytes=64) for a in range(PASSES)] for m in range(2)]
+        slots = {"wbf10": "wbf01", "wbf11": "pbf00", "gg0": "pbf00", "gg1": "pbf03", "gg2": "pbf10"}
+        made = {}
+
+        def lazy(name, shape, dtype):
+            if name not in made:
+                made[name] = keep.tile(shape, dtype, name=name, tag=slots.get(name, name), align_bytes=64)
+            return made[name]
+
+        def wbf(m, a):
+            return lazy(f"wbf{m}{a}", [P, 4, P, 4], BF16)
+
+        def pbf(m, s):
+            return lazy(f"pbf{m}{s}", [P, SL, 4], BF16)
+
+        def gg(i):
+            return lazy(f"gg{i}", [P, S], F32)
+
+        wq = [[keep.tile([P, H], U32, name=f"wq{m}{a}", align_bytes=64) for a in range(PASSES)] for m in range(2)]
+        wsc = [[keep.tile([P, H], U8, name=f"wsc{m}{a}", align_bytes=64) for a in range(PASSES)] for m in range(2)]
+        pq = [keep.tile([P, S], U32, name=f"pq{m}", align_bytes=64) for m in range(2)]
+        psc = [keep.tile([P, S], U8, name=f"psc{m}", align_bytes=64) for m in range(2)]
+        wmw = keep.tile([P, 2 * N], U8, name="wmw", align_bytes=64)
+        wms = keep.tile([P, N // 4], I32, name="wms", align_bytes=64)
+        g = [keep.tile([P, T], F32, name=f"g{i}", align_bytes=64) for i in range(NT)]
+        lg = keep.tile([P, NT, S], F32, name="lg", align_bytes=64)
+        res = keep.tile([P, NT, S], F32, name="res", align_bytes=64)
+        warm = keep.tile([P, 16], F32, name="warm", align_bytes=64)
+
+        w_in = (wc, ws)
+
+        def load_tab(a):
+            nc.sync.dma_start(out=tabw[a][:], in_=tab_words[a].rearrange("p t i -> p (t i)").bitcast(I32))
+
+        def load_w(m, a):
+            nc.sync.dma_start(out=wraw[m][a][:], in_=w_in[m][512 * a : 512 * (a + 1), :].rearrange("(p j) c -> p j c", j=4))
+
+        def load_g(i):
+            nc.sync.dma_start(out=g[i][:], in_=gT[P * i : P * (i + 1), :])
+
+        def load_tab_scales(eng):
+            for q in range(4):
+                eng.dma_start(out=tabs[32 * q : 32 * q + 8, :], in_=tab_scales[:, 4 * q : 4 * q + 4, :].bitcast(I32))
+
+        def load_wm(eng):
+            eng.dma_start(out=wmw[:].bitcast(I32), in_=wm_words[0].bitcast(I32))
+            for q in range(4):
+                eng.dma_start(out=wms[32 * q : 32 * q + 4, :], in_=wm_scales[0, 4 * q : 4 * q + 4, :].bitcast(I32))
+
+        def offs_sl(lo, n):
+            return offsets[:, lo // 16 : (lo + n) // 16]
+
+        def gather_tab(a, lo, n):
+            nc.vector.tensor_copy(out=vw[a][:, lo : lo + n], in_=tabw[a][:].bitcast(U32).indirect(offs_sl(lo, n)))
+
+        def gather_scales(lo, n):
+            nc.vector.tensor_copy(out=vs[:, lo : lo + n], in_=tabs[:].bitcast(U8).indirect(offs_sl(lo, n)))
+
+        def gather_g(i, lo, n):
+            nc.vector.tensor_copy(out=gg(i)[:, lo : lo + n], in_=g[i][:].indirect(offs_sl(lo, n)))
+
+        def cast_w(eng, m, a, lo, hi):
+            src = wraw[m][a][:].rearrange("p j (m t) -> p m j t", t=4)[:, lo:hi]
+            dst = wbf(m, a)[:].rearrange("p t m j -> p m j t")[:, lo:hi]
+            if eng == "v":
+                nc.vector.tensor_copy(out=dst, in_=src)
+            elif eng == "s":
+                nc.scalar.activation(out=dst, in_=src, func=ACT.Copy)
+            else:
+                nc.gpsimd.tensor_scalar(out=dst, in0=src, scalar1=1.0, scalar2=0.0, op0=ALU.mult, op1=ALU.add)
+
+        def quant_w(m, a):
+            nc.vector.quantize_mx(out=wq[m][a][:].bitcast(FP8X4), scales=wsc[m][a][:], in_=wbf(m, a)[:].rearrange("p t m j -> p (t m j)"))
+
+        def stage1(m, b):
+            cols = slice(BLK * b, BLK * (b + 1))
+            acc = psum.tile([P, 4, BLK], F32, name="acc1", tag="bank")
+            for t in range(4):
+                wcols = slice(P * t, P * (t + 1))
+                for a in range(PASSES):
+                    nc.tensor.matmul_mx(
+                        out=acc[:, t, :],
+                        lhsT=wq[m][a][:, wcols].bitcast(FP8X4),
+                        lhsT_scale=wsc[m][a][:, wcols],
+                        rhs=vw[a][:, cols].bitcast(FP8X4),
+                        rhs_scale=vs[4 * a : P, cols],
+                        start=(a == 0),
+                        stop=(a == PASSES - 1),
+                    )
+            nc.scalar.activation(out=pbf(m, b // 2)[:, BLK * (b % 2) : BLK * (b % 2 + 1), :], in_=acc[:].rearrange("p t j -> p j t"), func=ACT.Square)
+
+        def quant_p(m, s):
+            cols = slice(SL * s, SL * (s + 1))
+            nc.vector.quantize_mx(out=pq[m][:, cols].bitcast(FP8X4), scales=psc[m][:, cols], in_=pbf(m, s)[:].rearrange("p j t -> p (j t)"))
+
+        def stage2(h, i):
+            cols = slice(512 * h, 512 * (h + 1))
+            acc = psum.tile([P, 512], F32, name="acc2", tag="bank")
+            for m in range(2):
+                nc.tensor.matmul_mx(
+                    out=acc[:],
+                    lhsT=wmw[:, 2 * P * i : 2 * P * (i + 1)].bitcast(FP4X4),
+                    lhsT_scale=wms[:].bitcast(U8)[:, P * i : P * (i + 1)],
+                    rhs=pq[m][:, cols].bitcast(FP8X4),
+                    rhs_scale=psc[m][:, cols],
+                    start=(m == 0),
+                    stop=(m == 1),
+                )
+            nc.scalar.activation(out=lg[:, i, cols], in_=acc[:], func=ACT.Ln, bias=1.0)
+
+        def sub(eng, i, lo, n):
+            e = nc.vector if eng == "v" else nc.gpsimd
+            e.tensor_tensor(out=res[:, i, lo : lo + n], in0=lg[:, i, lo : lo + n], in1=gg(i)[:, lo : lo + n], op=ALU.subtract)
+
+        def store(i, lo, n):
+            nc.sync.dma_start(out=out[P * i : P * (i + 1), lo : lo + n], in_=res[:, i, lo : lo + n])
+
+        nc.sync.dma_start(offsets[:], offs)
+        nc.vector.memset(tabs[:], 0)
+        nc.vector.memset(wms[:], 0)
+        nc.vector.memset(warm[:, 0:8], 1.0)
+        load_tab_scales(nc.scalar)
+        nc.scalar.activation(out=warm[:, 8:16], in_=warm[:, 0:8], func=ACT.Ln)
+        load_tab(0)
+        load_w(0, 0)
+        load_w(0, 1)
+        load_tab(1)
+        load_w(1, 0)
+        load_w(1, 1)
+        load_g(0)
+        load_wm(nc.sync)
+        load_g(1)
+        load_g(2)
+
+        for h in range(2):
+            gather_tab(0, 512 * h, 512)
+        for h in range(2):
+            gather_scales(512 * h, 512)
+        cast_w("s", 0, 0, 0, 128)
+        quant_w(0, 0)
+        cast_w("s", 0, 1, 0, 48)
+        cast_w("v", 0, 1, 48, 128)
+        quant_w(0, 1)
+        for s in range(NSL):
+            gather_tab(1, SL * s, SL)
+        stage1(0, 0)
+        stage1(0, 1)
+        cast_w("s", 1, 0, 0, 32)
+        cast_w("v", 1, 0, 32, 128)
+        quant_w(1, 0)
+        quant_p(0, 0)
+        stage1(0, 2)
+        stage1(0, 3)
+        cast_w("s", 1, 1, 0, 48)
+        cast_w("v", 1, 1, 48, 128)
+        quant_w(1, 1)
+        quant_p(0, 1)
+        for s in range(2, NSL):
+            stage1(0, 2 * s)
+            stage1(0, 2 * s + 1)
+            quant_p(0, s)
+        for s in range(3):
+            stage1(1, 2 * s)
+            stage1(1, 2 * s + 1)
+            quant_p(1, s)
+        stage2(0, 0)
+        stage1(1, 6)
+        stage2(0, 1)
+        stage1(1, 7)
+        quant_p(1, 3)
+        stage2(0, 2)
+        for i in range(NT):
+            stage2(1, i)
+        for s in range(NSL):
+            gather_g(0, SL * s, SL)
+        for s in range(2):
+            gather_g(1, SL * s, SL)
+        for i in range(2):
+            sub("v", i, 0, 512)
+            store(i, 0, 512)
+        for s in range(2, NSL):
+            gather_g(1, SL * s, SL)
+        for s in range(2):
+            gather_g(2, SL * s, SL)
+        sub("v", 2, 0, 512)
+        store(2, 0, 512)
+        for i in range(2):
+            sub("v", i, 512, 512)
+            store(i, 512, 512)
+        for s in range(2, NSL):
+            gather_g(2, SL * s, SL)
+            sub("v", 2, SL * s, SL)
+            store(2, SL * s, SL)

@@ -29,59 +29,72 @@ def tile_list_voiced_log_spectra_kernel(tc, tab_words, tab_scales, offs, wc, ws,
     nc = tc.nc
     with ExitStack() as ctx:
         keep = ctx.enter_context(tc.tile_pool(name="keep", bufs=1))
-        psum = ctx.enter_context(tc.psum_pool(name="psum", bufs=8))
+        work = ctx.enter_context(tc.tile_pool(name="work", bufs=1))
+        psa = ctx.enter_context(tc.psum_pool(name="psa", bufs=3))
+        psb = ctx.enter_context(tc.psum_pool(name="psb", bufs=5))
 
         offsets = keep.tile([P, S // 16], U16, name="offsets")
-        tabw = [keep.tile([P, T], I32, name=f"tabw{a}", align_bytes=64) for a in range(PASSES)]
         tabs = keep.tile([P, T // 4], I32, name="tabs", align_bytes=64)
-        vw = [keep.tile([P, S], U32, name=f"vw{a}", align_bytes=64) for a in range(PASSES)]
         vs = keep.tile([P, S], U8, name="vs", align_bytes=64)
-        wraw = [[keep.tile([P, 4, H], F32, name=f"wraw{m}{a}", align_bytes=64) for a in range(PASSES)] for m in range(2)]
-        slots = {"wbf10": "wbf01", "wbf11": "pbf00", "gg0": "pbf00", "gg1": "pbf03", "gg2": "pbf10"}
-        made = {}
-
-        def lazy(name, shape, dtype):
-            if name not in made:
-                made[name] = keep.tile(shape, dtype, name=name, tag=slots.get(name, name), align_bytes=64)
-            return made[name]
-
-        def wbf(m, a):
-            return lazy(f"wbf{m}{a}", [P, 4, P, 4], BF16)
-
-        def pbf(m, s):
-            return lazy(f"pbf{m}{s}", [P, SL, 4], BF16)
-
-        def gg(i):
-            return lazy(f"gg{i}", [P, S], F32)
-
         wq = [[keep.tile([P, H], U32, name=f"wq{m}{a}", align_bytes=64) for a in range(PASSES)] for m in range(2)]
         wsc = [[keep.tile([P, H], U8, name=f"wsc{m}{a}", align_bytes=64) for a in range(PASSES)] for m in range(2)]
         pq = [keep.tile([P, S], U32, name=f"pq{m}", align_bytes=64) for m in range(2)]
         psc = [keep.tile([P, S], U8, name=f"psc{m}", align_bytes=64) for m in range(2)]
         wmw = keep.tile([P, 2 * N], U8, name="wmw", align_bytes=64)
-        wms = keep.tile([P, N // 4], I32, name="wms", align_bytes=64)
-        g = [keep.tile([P, T], F32, name=f"g{i}", align_bytes=64) for i in range(NT)]
         lg = keep.tile([P, NT, S], F32, name="lg", align_bytes=64)
         res = keep.tile([P, NT, S], F32, name="res", align_bytes=64)
-        warm = keep.tile([P, 16], F32, name="warm", align_bytes=64)
+
+        place = {"warm": 0, "wraw00": 0, "wraw01": 8, "tabw1": 16, "wraw10": 24, "wraw11": 32, "g0": 40, "g1": 48, "g2": 56, "wms": 64, "tabw0": 65, "vw0": 73, "wbf00": 77, "wbf01": 81, "vw1": 8, "wbf10": 12, "wbf11": 24, "gg0": 32, "gg1": 36, "pbf00": 85, "pbf01": 89, "pbf10": 93, "gg2": 93, "pbf11": 97}
+        made = {}
+
+        def lazy(name, shape, dtype):
+            if name not in made:
+                made[name] = work.tile(shape, dtype, name=name, offset=1024 * place[name], align_bytes=64)
+            return made[name]
+
+        def tabw(a):
+            return lazy(f"tabw{a}", [P, T], I32)
+
+        def wraw(m, a):
+            return lazy(f"wraw{m}{a}", [P, 4, H], F32)
+
+        def g(i):
+            return lazy(f"g{i}", [P, T], F32)
+
+        def wbf(m, a):
+            return lazy(f"wbf{m}{a}", [P, 4, P, 4], BF16)
+
+        def pbf(m, h):
+            return lazy(f"pbf{m}{h}", [P, 512, 4], BF16)
+
+        def gg(i):
+            return lazy(f"gg{i}", [P, S], F32)
+
+        def vw(a):
+            return lazy(f"vw{a}", [P, S], U32)
+
+        warm = lazy("warm", [P, 256 * 65], F32)
+        wms = lazy("wms", [P, N // 4], I32)
 
         w_in = (wc, ws)
 
         def load_tab(a):
-            nc.sync.dma_start(out=tabw[a][:], in_=tab_words[a].rearrange("p t i -> p (t i)").bitcast(I32))
+            nc.sync.dma_start(out=tabw(a)[:], in_=tab_words[a].rearrange("p t i -> p (t i)").bitcast(I32))
 
         def load_w(m, a):
-            nc.sync.dma_start(out=wraw[m][a][:], in_=w_in[m][512 * a : 512 * (a + 1), :].rearrange("(p j) c -> p j c", j=4))
+            nc.sync.dma_start(out=wraw(m, a)[:], in_=w_in[m][512 * a : 512 * (a + 1), :].rearrange("(p j) c -> p j c", j=4))
 
         def load_g(i):
-            nc.sync.dma_start(out=g[i][:], in_=gT[P * i : P * (i + 1), :])
+            nc.sync.dma_start(out=g(i)[:], in_=gT[P * i : P * (i + 1), :])
 
         def load_tab_scales(eng):
             for q in range(4):
                 eng.dma_start(out=tabs[32 * q : 32 * q + 8, :], in_=tab_scales[:, 4 * q : 4 * q + 4, :].bitcast(I32))
 
-        def load_wm(eng):
+        def load_wm_words(eng):
             eng.dma_start(out=wmw[:].bitcast(I32), in_=wm_words[0].bitcast(I32))
+
+        def load_wm(eng):
             for q in range(4):
                 eng.dma_start(out=wms[32 * q : 32 * q + 4, :], in_=wm_scales[0, 4 * q : 4 * q + 4, :].bitcast(I32))
 
@@ -89,16 +102,16 @@ def tile_list_voiced_log_spectra_kernel(tc, tab_words, tab_scales, offs, wc, ws,
             return offsets[:, lo // 16 : (lo + n) // 16]
 
         def gather_tab(a, lo, n):
-            nc.vector.tensor_copy(out=vw[a][:, lo : lo + n], in_=tabw[a][:].bitcast(U32).indirect(offs_sl(lo, n)))
+            nc.vector.tensor_copy(out=vw(a)[:, lo : lo + n], in_=tabw(a)[:].bitcast(U32).indirect(offs_sl(lo, n)))
 
         def gather_scales(lo, n):
             nc.vector.tensor_copy(out=vs[:, lo : lo + n], in_=tabs[:].bitcast(U8).indirect(offs_sl(lo, n)))
 
         def gather_g(i, lo, n):
-            nc.vector.tensor_copy(out=gg(i)[:, lo : lo + n], in_=g[i][:].indirect(offs_sl(lo, n)))
+            nc.vector.tensor_copy(out=gg(i)[:, lo : lo + n], in_=g(i)[:].indirect(offs_sl(lo, n)))
 
         def cast_w(eng, m, a, lo, hi):
-            src = wraw[m][a][:].rearrange("p j (m t) -> p m j t", t=4)[:, lo:hi]
+            src = wraw(m, a)[:].rearrange("p j (m t) -> p m j t", t=4)[:, lo:hi]
             dst = wbf(m, a)[:].rearrange("p t m j -> p m j t")[:, lo:hi]
             if eng == "v":
                 nc.vector.tensor_copy(out=dst, in_=src)
@@ -112,7 +125,7 @@ def tile_list_voiced_log_spectra_kernel(tc, tab_words, tab_scales, offs, wc, ws,
 
         def stage1(m, b):
             cols = slice(BLK * b, BLK * (b + 1))
-            acc = psum.tile([P, 4, BLK], F32, name="acc1", tag="bank")
+            acc = (psa, psb)[m].tile([P, 4, BLK], F32, name="acc1", tag="bank")
             for t in range(4):
                 wcols = slice(P * t, P * (t + 1))
                 for a in range(PASSES):
@@ -120,20 +133,33 @@ def tile_list_voiced_log_spectra_kernel(tc, tab_words, tab_scales, offs, wc, ws,
                         out=acc[:, t, :],
                         lhsT=wq[m][a][:, wcols].bitcast(FP8X4),
                         lhsT_scale=wsc[m][a][:, wcols],
-                        rhs=vw[a][:, cols].bitcast(FP8X4),
+                        rhs=vw(a)[:, cols].bitcast(FP8X4),
                         rhs_scale=vs[4 * a : P, cols],
                         start=(a == 0),
                         stop=(a == PASSES - 1),
                     )
-            nc.scalar.activation(out=pbf(m, b // 2)[:, BLK * (b % 2) : BLK * (b % 2 + 1), :], in_=acc[:].rearrange("p t j -> p j t"), func=ACT.Square)
+            nc.scalar.activation(out=pbf(m, b // 4)[:, BLK * (b % 4) : BLK * (b % 4 + 1), :], in_=acc[:].rearrange("p t j -> p j t"), func=ACT.Square)
 
-        def quant_p(m, s):
-            cols = slice(SL * s, SL * (s + 1))
-            nc.vector.quantize_mx(out=pq[m][:, cols].bitcast(FP8X4), scales=psc[m][:, cols], in_=pbf(m, s)[:].rearrange("p j t -> p (j t)"))
+        def warm_pe(n):
+            acc = psa.tile([P, 512], F32, name="accw", tag="bank")
+            for r in range(n):
+                nc.tensor.matmul_mx(
+                    out=acc[:],
+                    lhsT=wq[0][0][:, 0:P].bitcast(FP8X4),
+                    lhsT_scale=wsc[0][0][:, 0:P],
+                    rhs=vw(0)[:, 0:512].bitcast(FP8X4),
+                    rhs_scale=vs[:, 0:512],
+                    start=True,
+                    stop=True,
+                )
+
+        def quant_p(m, h):
+            cols = slice(512 * h, 512 * (h + 1))
+            nc.vector.quantize_mx(out=pq[m][:, cols].bitcast(FP8X4), scales=psc[m][:, cols], in_=pbf(m, h)[:].rearrange("p j t -> p (j t)"))
 
         def stage2(h, i):
             cols = slice(512 * h, 512 * (h + 1))
-            acc = psum.tile([P, 512], F32, name="acc2", tag="bank")
+            acc = psa.tile([P, 512], F32, name="acc2", tag="bank")
             for m in range(2):
                 nc.tensor.matmul_mx(
                     out=acc[:],
@@ -155,11 +181,12 @@ def tile_list_voiced_log_spectra_kernel(tc, tab_words, tab_scales, offs, wc, ws,
 
         nc.sync.dma_start(offsets[:], offs)
         nc.vector.memset(tabs[:], 0)
-        nc.vector.memset(wms[:], 0)
         nc.vector.memset(warm[:, 0:8], 1.0)
-        load_tab_scales(nc.scalar)
         nc.scalar.activation(out=warm[:, 8:16], in_=warm[:, 0:8], func=ACT.Ln)
+        nc.vector.memset(wms[:], 0)
         load_tab(0)
+        load_tab_scales(nc.sync)
+        load_wm_words(nc.sync)
         load_w(0, 0)
         load_w(0, 1)
         load_tab(1)
@@ -170,62 +197,40 @@ def tile_list_voiced_log_spectra_kernel(tc, tab_words, tab_scales, offs, wc, ws,
         load_g(1)
         load_g(2)
 
-        for h in range(2):
-            gather_tab(0, 512 * h, 512)
-        for h in range(2):
-            gather_scales(512 * h, 512)
+        gather_tab(0, 0, S)
+        gather_scales(0, S)
         cast_w("s", 0, 0, 0, 128)
-        quant_w(0, 0)
         cast_w("s", 0, 1, 0, 48)
         cast_w("v", 0, 1, 48, 128)
+        quant_w(0, 0)
         quant_w(0, 1)
-        for s in range(NSL):
-            gather_tab(1, SL * s, SL)
-        stage1(0, 0)
-        stage1(0, 1)
-        cast_w("s", 1, 0, 0, 32)
-        cast_w("v", 1, 0, 32, 128)
+        warm_pe(3)
+        gather_tab(1, 0, 256)
+        gather_tab(1, 256, 256)
+        gather_tab(1, 512, 512)
+        cast_w("v", 1, 0, 0, 128)
         quant_w(1, 0)
+        for b in range(4):
+            stage1(0, b)
+        cast_w("s", 1, 1, 0, 64)
+        cast_w("v", 1, 1, 64, 128)
         quant_p(0, 0)
-        stage1(0, 2)
-        stage1(0, 3)
-        cast_w("s", 1, 1, 0, 48)
-        cast_w("v", 1, 1, 48, 128)
         quant_w(1, 1)
+        for b in range(4, 8):
+            stage1(0, b)
         quant_p(0, 1)
-        for s in range(2, NSL):
-            stage1(0, 2 * s)
-            stage1(0, 2 * s + 1)
-            quant_p(0, s)
-        for s in range(3):
-            stage1(1, 2 * s)
-            stage1(1, 2 * s + 1)
-            quant_p(1, s)
-        stage2(0, 0)
-        stage1(1, 6)
-        stage2(0, 1)
-        stage1(1, 7)
-        quant_p(1, 3)
-        stage2(0, 2)
-        for i in range(NT):
-            stage2(1, i)
-        for s in range(NSL):
-            gather_g(0, SL * s, SL)
-        for s in range(2):
-            gather_g(1, SL * s, SL)
-        for i in range(2):
-            sub("v", i, 0, 512)
-            store(i, 0, 512)
-        for s in range(2, NSL):
-            gather_g(1, SL * s, SL)
-        for s in range(2):
-            gather_g(2, SL * s, SL)
-        sub("v", 2, 0, 512)
-        store(2, 0, 512)
-        for i in range(2):
-            sub("v", i, 512, 512)
-            store(i, 512, 512)
-        for s in range(2, NSL):
-            gather_g(2, SL * s, SL)
-            sub("v", 2, SL * s, SL)
-            store(2, SL * s, SL)
+        for h in range(2):
+            for b in range(4 * h, 4 * h + 4):
+                stage1(1, b)
+            quant_p(1, h)
+        for h in range(2):
+            for i in range(NT):
+                stage2(h, i)
+        gather_g(0, 0, S)
+        gather_g(1, 0, S)
+        gather_g(2, 0, 512)
+        gather_g(2, 512, 512)
+        for h in range(2):
+            for i in range(NT):
+                sub("v", i, 512 * h, 512)
+                store(i, 512 * h, 512)

@@ -34,17 +34,16 @@ def tile_list_voiced_log_spectra_kernel(tc, tab_words, tab_scales, offs, wc, ws,
         psb = ctx.enter_context(tc.psum_pool(name="psb", bufs=5))
 
         offsets = keep.tile([P, S // 16], U16, name="offsets")
-        tabs = keep.tile([P, T // 4], I32, name="tabs", align_bytes=64)
         vs = keep.tile([P, S], U8, name="vs", align_bytes=64)
         wq = [[keep.tile([P, H], U32, name=f"wq{m}{a}", align_bytes=64) for a in range(PASSES)] for m in range(2)]
-        wsc = [[keep.tile([P, H], U8, name=f"wsc{m}{a}", align_bytes=64) for a in range(PASSES)] for m in range(2)]
+        wsc_keep = {(m, a): keep.tile([P, H], U8, name=f"wsc{m}{a}", align_bytes=64) for a in range(PASSES) for m in range(2) if (m, a) != (0, 0)}
         pq = [keep.tile([P, S], U32, name=f"pq{m}", align_bytes=64) for m in range(2)]
         psc = [keep.tile([P, S], U8, name=f"psc{m}", align_bytes=64) for m in range(2)]
         wmw = keep.tile([P, 2 * N], U8, name="wmw", align_bytes=64)
         lg = keep.tile([P, NT, S], F32, name="lg", align_bytes=64)
         res = keep.tile([P, NT, S], F32, name="res", align_bytes=64)
 
-        place = {"warm": 0, "wraw00": 0, "wraw01": 8, "tabw1": 16, "wraw10": 24, "wraw11": 32, "g0": 40, "g1": 48, "g2": 56, "wms": 64, "tabw0": 65, "vw0": 73, "wbf00": 77, "wbf01": 81, "vw1": 8, "wbf10": 12, "wbf11": 24, "gg0": 32, "gg1": 36, "pbf00": 85, "pbf01": 89, "pbf10": 93, "gg2": 93, "pbf11": 97}
+        place = {"warm": 104, "wraw00": 0, "wraw01": 8, "tabw1": 16, "wraw10": 24, "wraw11": 32, "g0": 40, "g1": 48, "g2": 56, "wms": 101, "tabw0": 64, "vw0": 72, "wbf00": 76, "wbf01": 81, "vw1": 8, "wbf10": 12, "wbf11": 24, "gg0": 32, "gg1": 36, "pbf00": 85, "pbf01": 89, "pbf10": 93, "gg2": 93, "pbf11": 97, "tabs": 80, "wsc00": 80}
         made = {}
 
         def lazy(name, shape, dtype):
@@ -73,7 +72,11 @@ def tile_list_voiced_log_spectra_kernel(tc, tab_words, tab_scales, offs, wc, ws,
         def vw(a):
             return lazy(f"vw{a}", [P, S], U32)
 
-        warm = lazy("warm", [P, 256 * 65], F32)
+        def wsc(m, a):
+            return lazy("wsc00", [P, H], U8) if (m, a) == (0, 0) else wsc_keep[(m, a)]
+
+        tabs = lazy("tabs", [P, T // 4], I32)
+        warm = lazy("warm", [P, 256 * 1], F32)
         wms = lazy("wms", [P, N // 4], I32)
 
         w_in = (wc, ws)
@@ -121,7 +124,7 @@ def tile_list_voiced_log_spectra_kernel(tc, tab_words, tab_scales, offs, wc, ws,
                 nc.gpsimd.tensor_scalar(out=dst, in0=src, scalar1=1.0, scalar2=0.0, op0=ALU.mult, op1=ALU.add)
 
         def quant_w(m, a):
-            nc.vector.quantize_mx(out=wq[m][a][:].bitcast(FP8X4), scales=wsc[m][a][:], in_=wbf(m, a)[:].rearrange("p t m j -> p (t m j)"))
+            nc.vector.quantize_mx(out=wq[m][a][:].bitcast(FP8X4), scales=wsc(m, a)[:], in_=wbf(m, a)[:].rearrange("p t m j -> p (t m j)"))
 
         def stage1(m, b):
             cols = slice(BLK * b, BLK * (b + 1))
@@ -132,7 +135,7 @@ def tile_list_voiced_log_spectra_kernel(tc, tab_words, tab_scales, offs, wc, ws,
                     nc.tensor.matmul_mx(
                         out=acc[:, t, :],
                         lhsT=wq[m][a][:, wcols].bitcast(FP8X4),
-                        lhsT_scale=wsc[m][a][:, wcols],
+                        lhsT_scale=wsc(m, a)[:, wcols],
                         rhs=vw(a)[:, cols].bitcast(FP8X4),
                         rhs_scale=vs[4 * a : P, cols],
                         start=(a == 0),
@@ -146,7 +149,7 @@ def tile_list_voiced_log_spectra_kernel(tc, tab_words, tab_scales, offs, wc, ws,
                 nc.tensor.matmul_mx(
                     out=acc[:],
                     lhsT=wq[0][0][:, 0:P].bitcast(FP8X4),
-                    lhsT_scale=wsc[0][0][:, 0:P],
+                    lhsT_scale=wsc(0, 0)[:, 0:P],
                     rhs=vw(0)[:, 0:512].bitcast(FP8X4),
                     rhs_scale=vs[:, 0:512],
                     start=True,
@@ -184,18 +187,18 @@ def tile_list_voiced_log_spectra_kernel(tc, tab_words, tab_scales, offs, wc, ws,
         nc.vector.memset(warm[:, 0:8], 1.0)
         nc.scalar.activation(out=warm[:, 8:16], in_=warm[:, 0:8], func=ACT.Ln)
         nc.vector.memset(wms[:], 0)
+        load_tab_scales(nc.gpsimd)
         load_tab(0)
-        load_tab_scales(nc.sync)
-        load_wm_words(nc.sync)
         load_w(0, 0)
         load_w(0, 1)
         load_tab(1)
         load_w(1, 0)
         load_w(1, 1)
         load_g(0)
-        load_wm(nc.sync)
         load_g(1)
         load_g(2)
+        load_wm_words(nc.gpsimd)
+        load_wm(nc.gpsimd)
 
         gather_tab(0, 0, S)
         gather_scales(0, S)

@@ -43,7 +43,8 @@ def tile_list_voiced_log_spectra_kernel(tc, tab_words, tab_scales, offs, wc, ws,
         lg = keep.tile([P, NT, S], F32, name="lg", align_bytes=64)
         res = keep.tile([P, NT, S], F32, name="res", align_bytes=64)
 
-        place = {"warm": 104, "wraw00": 0, "wraw01": 8, "tabw1": 16, "wraw10": 24, "wraw11": 32, "g0": 40, "g1": 48, "g2": 56, "wms": 101, "tabw0": 64, "vw0": 72, "wbf00": 76, "wbf01": 81, "vw1": 8, "wbf10": 12, "wbf11": 24, "gg0": 32, "gg1": 36, "pbf00": 85, "pbf01": 89, "pbf10": 93, "gg2": 93, "pbf11": 97, "tabs": 80, "wsc00": 80}
+        one = keep.tile([P, 16], F32, name="one", align_bytes=64)
+        place = {"warm": 0, "wraw00": 0, "wraw01": 8, "tabw1": 16, "wraw10": 24, "wraw11": 32, "g0": 40, "g1": 48, "g2": 56, "wms": 64, "tabw0": 65, "vw0": 73, "wbf00": 77, "wbf01": 82, "vw1": 8, "wbf10": 12, "wbf11": 24, "gg0": 32, "gg1": 36, "pbf00": 86, "pbf01": 90, "pbf10": 94, "gg2": 94, "pbf11": 98, "tabs": 81, "wsc00": 81}
         made = {}
 
         def lazy(name, shape, dtype):
@@ -76,7 +77,7 @@ def tile_list_voiced_log_spectra_kernel(tc, tab_words, tab_scales, offs, wc, ws,
             return lazy("wsc00", [P, H], U8) if (m, a) == (0, 0) else wsc_keep[(m, a)]
 
         tabs = lazy("tabs", [P, T // 4], I32)
-        warm = lazy("warm", [P, 256 * 1], F32)
+        warm = lazy("warm", [P, 256 * 65], F32)
         wms = lazy("wms", [P, N // 4], I32)
 
         w_in = (wc, ws)
@@ -90,9 +91,14 @@ def tile_list_voiced_log_spectra_kernel(tc, tab_words, tab_scales, offs, wc, ws,
         def load_g(i):
             nc.sync.dma_start(out=g(i)[:], in_=gT[P * i : P * (i + 1), :])
 
-        def load_tab_scales(eng):
-            for q in range(4):
-                eng.dma_start(out=tabs[32 * q : 32 * q + 8, :], in_=tab_scales[:, 4 * q : 4 * q + 4, :].bitcast(I32))
+        def load_tab_scales_pool():
+            for q in range(2):
+                nc.gpsimd.dma_start(out=tabs[32 * q : 32 * q + 8, :], in_=tab_scales[:, 4 * q : 4 * q + 4, :].bitcast(I32))
+
+        def load_tab_scales_sync():
+            for q in range(2, 4):
+                for a in range(PASSES):
+                    nc.sync.dma_start(out=tabs[32 * q + 4 * a : 32 * q + 4 * a + 4, :], in_=tab_scales[a, 4 * q : 4 * q + 4, :].bitcast(I32))
 
         def load_wm_words(eng):
             eng.dma_start(out=wmw[:].bitcast(I32), in_=wm_words[0].bitcast(I32))
@@ -173,7 +179,7 @@ def tile_list_voiced_log_spectra_kernel(tc, tab_words, tab_scales, offs, wc, ws,
                     start=(m == 0),
                     stop=(m == 1),
                 )
-            nc.scalar.activation(out=lg[:, i, cols], in_=acc[:], func=ACT.Ln, bias=1.0)
+            nc.scalar.activation(out=lg[:, i, cols], in_=acc[:], func=ACT.Ln, bias=one[:, 0:1])
 
         def sub(eng, i, lo, n):
             e = nc.vector if eng == "v" else nc.gpsimd
@@ -185,20 +191,22 @@ def tile_list_voiced_log_spectra_kernel(tc, tab_words, tab_scales, offs, wc, ws,
         nc.sync.dma_start(offsets[:], offs)
         nc.vector.memset(tabs[:], 0)
         nc.vector.memset(warm[:, 0:8], 1.0)
-        nc.scalar.activation(out=warm[:, 8:16], in_=warm[:, 0:8], func=ACT.Ln)
+        nc.vector.tensor_copy(out=one[:, 0:8], in_=warm[:, 0:8])
+        nc.scalar.activation(out=one[:, 8:16], in_=one[:, 0:8], func=ACT.Ln)
         nc.vector.memset(wms[:], 0)
-        load_tab_scales(nc.gpsimd)
+        load_tab_scales_pool()
         load_tab(0)
+        load_tab_scales_sync()
+        load_wm_words(nc.sync)
         load_w(0, 0)
         load_w(0, 1)
         load_tab(1)
         load_w(1, 0)
         load_w(1, 1)
         load_g(0)
+        load_wm(nc.sync)
         load_g(1)
         load_g(2)
-        load_wm_words(nc.gpsimd)
-        load_wm(nc.gpsimd)
 
         gather_tab(0, 0, S)
         gather_scales(0, S)

@@ -17,12 +17,37 @@ ACT = mybir.ActivationFunctionType
 ALU = mybir.AluOpType
 
 P = 128
-PASSES = 2
-BLK = 128
-NBLK = S // BLK
-SL = 256
-NSL = S // SL
-NT = N // P
+PACK = 4
+K_PASS = P * PACK
+PASSES = K // K_PASS
+COS, SIN = 0, 1
+BLOCK = 128
+HALF = 512
+BLOCKS_PER_HALF = HALF // BLOCK
+BAND_TILES = N // P
+QUADRANTS = 4
+LIST_ROWS = 16
+ONES = 8
+
+COS_BANKS, SIN_BANKS = 3, 5
+
+SCALAR_SHARE = {(COS, 0): 128, (COS, 1): 48, (SIN, 0): 0, (SIN, 1): 64}
+
+SECOND_PASS_SLICES = ((0, 256), (256, 256), (512, 512))
+
+SEED_KIB = 66
+PLACE = {
+    "seed": 0,
+    "w_raw00": 0, "w_raw01": 8, "tab_word1": 16, "w_raw10": 24, "w_raw11": 32,
+    "floor0": 40, "floor1": 48, "floor2": 56, "wm_scale": 64, "wm_word": 65,
+    "tab_word0": 66, "v_word0": 74, "w_bf00": 78, "tab_scale": 82,
+    "sq_bf00": 87, "sq_bf01": 91, "sq_bf10": 95, "sq_bf11": 99,
+    "w_scale00": 82, "w_bf01": 83,
+    "v_word1": 8, "w_bf10": 12,
+    "w_bf11": 24,
+    "picked0": 32, "picked1": 36,
+    "picked2": 95,
+}
 
 
 def tile_list_voiced_log_spectra_kernel(tc, tab_words, tab_scales, offs, wc, ws, wm_words, wm_scales, gT, out):
@@ -30,218 +55,211 @@ def tile_list_voiced_log_spectra_kernel(tc, tab_words, tab_scales, offs, wc, ws,
     with ExitStack() as ctx:
         keep = ctx.enter_context(tc.tile_pool(name="keep", bufs=1))
         work = ctx.enter_context(tc.tile_pool(name="work", bufs=1))
-        psa = ctx.enter_context(tc.psum_pool(name="psa", bufs=3))
-        psb = ctx.enter_context(tc.psum_pool(name="psb", bufs=5))
+        cos_psum = ctx.enter_context(tc.psum_pool(name="cos_psum", bufs=COS_BANKS))
+        sin_psum = ctx.enter_context(tc.psum_pool(name="sin_psum", bufs=SIN_BANKS))
 
-        offsets = keep.tile([P, S // 16], U16, name="offsets")
-        vs = keep.tile([P, S], U8, name="vs", align_bytes=64)
-        wq = [[keep.tile([P, H], U32, name=f"wq{m}{a}", align_bytes=64) for a in range(PASSES)] for m in range(2)]
-        wsc_keep = {(m, a): keep.tile([P, H], U8, name=f"wsc{m}{a}", align_bytes=64) for a in range(PASSES) for m in range(2) if (m, a) != (0, 0)}
-        pq = [keep.tile([P, S], U32, name=f"pq{m}", align_bytes=64) for m in range(2)]
-        psc = [keep.tile([P, S], U8, name=f"psc{m}", align_bytes=64) for m in range(2)]
-        wmw = keep.tile([P, 2 * N], U8, name="wmw", align_bytes=64)
-        lg = keep.tile([P, NT, S], F32, name="lg", align_bytes=64)
-        res = keep.tile([P, NT, S], F32, name="res", align_bytes=64)
+        offsets = keep.tile([P, S // LIST_ROWS], U16, name="offsets")
+        v_scale = keep.tile([P, S], U8, name="v_scale", align_bytes=64)
+        w_word = [[keep.tile([P, H], U32, name=f"w_word{f}{a}", align_bytes=64) for a in range(PASSES)] for f in (COS, SIN)]
+        w_scale_kept = {
+            (f, a): keep.tile([P, H], U8, name=f"w_scale{f}{a}", align_bytes=64)
+            for a in range(PASSES)
+            for f in (COS, SIN)
+            if (f, a) != (COS, 0)
+        }
+        sq_word = [keep.tile([P, S], U32, name=f"sq_word{f}", align_bytes=64) for f in (COS, SIN)]
+        sq_scale = [keep.tile([P, S], U8, name=f"sq_scale{f}", align_bytes=64) for f in (COS, SIN)]
+        logs = keep.tile([P, BAND_TILES, S], F32, name="logs", align_bytes=64)
+        result = keep.tile([P, BAND_TILES, S], F32, name="result", align_bytes=64)
+        one = keep.tile([P, ONES], F32, name="one", align_bytes=64)
 
-        one = keep.tile([P, 16], F32, name="one", align_bytes=64)
-        place = {"warm": 0, "wraw00": 0, "wraw01": 8, "tabw1": 16, "wraw10": 24, "wraw11": 32, "g0": 40, "g1": 48, "g2": 56, "wms": 64, "tabw0": 65, "vw0": 73, "wbf00": 77, "wbf01": 82, "vw1": 8, "wbf10": 12, "wbf11": 24, "gg0": 32, "gg1": 36, "pbf00": 86, "pbf01": 90, "pbf10": 94, "gg2": 94, "pbf11": 98, "tabs": 81, "wsc00": 81}
         made = {}
 
-        def lazy(name, shape, dtype):
+        def placed(name, shape, dtype):
             if name not in made:
-                made[name] = work.tile(shape, dtype, name=name, offset=1024 * place[name], align_bytes=64)
+                made[name] = work.tile(shape, dtype, name=name, offset=1024 * PLACE[name], align_bytes=64)
             return made[name]
 
-        def tabw(a):
-            return lazy(f"tabw{a}", [P, T], I32)
+        def tab_word(a):
+            return placed(f"tab_word{a}", [P, T], I32)
 
-        def wraw(m, a):
-            return lazy(f"wraw{m}{a}", [P, 4, H], F32)
+        def w_raw(f, a):
+            return placed(f"w_raw{f}{a}", [P, PACK, H], F32)
 
-        def g(i):
-            return lazy(f"g{i}", [P, T], F32)
+        def floor(i):
+            return placed(f"floor{i}", [P, T], F32)
 
-        def wbf(m, a):
-            return lazy(f"wbf{m}{a}", [P, 4, P, 4], BF16)
+        def w_bf(f, a):
+            return placed(f"w_bf{f}{a}", [P, PACK, P, PACK], BF16)
 
-        def pbf(m, h):
-            return lazy(f"pbf{m}{h}", [P, 512, 4], BF16)
+        def sq_bf(f, h):
+            return placed(f"sq_bf{f}{h}", [P, HALF, PACK], BF16)
 
-        def gg(i):
-            return lazy(f"gg{i}", [P, S], F32)
+        def picked(i):
+            return placed(f"picked{i}", [P, S], F32)
 
-        def vw(a):
-            return lazy(f"vw{a}", [P, S], U32)
+        def v_word(a):
+            return placed(f"v_word{a}", [P, S], U32)
 
-        def wsc(m, a):
-            return lazy("wsc00", [P, H], U8) if (m, a) == (0, 0) else wsc_keep[(m, a)]
+        def w_scale(f, a):
+            return placed("w_scale00", [P, H], U8) if (f, a) == (COS, 0) else w_scale_kept[(f, a)]
 
-        tabs = lazy("tabs", [P, T // 4], I32)
-        warm = lazy("warm", [P, 256 * 65], F32)
-        wms = lazy("wms", [P, N // 4], I32)
+        tab_scale = placed("tab_scale", [P, T // 4], I32)
+        seed = placed("seed", [P, SEED_KIB * 256], F32)
+        wm_word = placed("wm_word", [P, 2 * N], U8)
+        wm_scale = placed("wm_scale", [P, N // 4], I32)
 
-        w_in = (wc, ws)
+        def load_tab_words(a):
+            nc.sync.dma_start(out=tab_word(a)[:], in_=tab_words[a].rearrange("p t i -> p (t i)").bitcast(I32))
 
-        def load_tab(a):
-            nc.sync.dma_start(out=tabw(a)[:], in_=tab_words[a].rearrange("p t i -> p (t i)").bitcast(I32))
+        def load_w(f, a):
+            rows = (wc, ws)[f][K_PASS * a : K_PASS * (a + 1), :]
+            nc.sync.dma_start(out=w_raw(f, a)[:], in_=rows.rearrange("(p j) c -> p j c", j=PACK))
 
-        def load_w(m, a):
-            nc.sync.dma_start(out=wraw(m, a)[:], in_=w_in[m][512 * a : 512 * (a + 1), :].rearrange("(p j) c -> p j c", j=4))
+        def load_floor(i):
+            nc.sync.dma_start(out=floor(i)[:], in_=gT[P * i : P * (i + 1), :])
 
-        def load_g(i):
-            nc.sync.dma_start(out=g(i)[:], in_=gT[P * i : P * (i + 1), :])
-
-        def load_tab_scales_pool():
-            for q in range(2):
-                nc.gpsimd.dma_start(out=tabs[32 * q : 32 * q + 8, :], in_=tab_scales[:, 4 * q : 4 * q + 4, :].bitcast(I32))
-
-        def load_tab_scales_sync():
-            for q in range(2, 4):
+        def load_tab_scales():
+            for q in range(QUADRANTS // 2):
+                nc.sync.dma_start(out=tab_scale[32 * q : 32 * q + 8, :], in_=tab_scales[:, 4 * q : 4 * q + 4, :].bitcast(I32))
+            for q in range(QUADRANTS // 2, QUADRANTS):
                 for a in range(PASSES):
-                    nc.sync.dma_start(out=tabs[32 * q + 4 * a : 32 * q + 4 * a + 4, :], in_=tab_scales[a, 4 * q : 4 * q + 4, :].bitcast(I32))
+                    rows = slice(32 * q + 4 * a, 32 * q + 4 * a + 4)
+                    nc.sync.dma_start(out=tab_scale[rows, :], in_=tab_scales[a, 4 * q : 4 * q + 4, :].bitcast(I32))
 
-        def load_wm_words(eng):
-            eng.dma_start(out=wmw[:].bitcast(I32), in_=wm_words[0].bitcast(I32))
+        def load_wm():
+            nc.sync.dma_start(out=wm_word[:].bitcast(I32), in_=wm_words[0].bitcast(I32))
+            for q in range(QUADRANTS):
+                nc.sync.dma_start(out=wm_scale[32 * q : 32 * q + 4, :], in_=wm_scales[0, 4 * q : 4 * q + 4, :].bitcast(I32))
 
-        def load_wm(eng):
-            for q in range(4):
-                eng.dma_start(out=wms[32 * q : 32 * q + 4, :], in_=wm_scales[0, 4 * q : 4 * q + 4, :].bitcast(I32))
+        def list_slice(lo, n):
+            return offsets[:, lo // LIST_ROWS : (lo + n) // LIST_ROWS]
 
-        def offs_sl(lo, n):
-            return offsets[:, lo // 16 : (lo + n) // 16]
+        def gather_words(a, lo, n):
+            nc.vector.tensor_copy(out=v_word(a)[:, lo : lo + n], in_=tab_word(a)[:].bitcast(U32).indirect(list_slice(lo, n)))
 
-        def gather_tab(a, lo, n):
-            nc.vector.tensor_copy(out=vw(a)[:, lo : lo + n], in_=tabw(a)[:].bitcast(U32).indirect(offs_sl(lo, n)))
+        def gather_scales():
+            nc.vector.tensor_copy(out=v_scale[:, 0:S], in_=tab_scale[:].bitcast(U8).indirect(list_slice(0, S)))
 
-        def gather_scales(lo, n):
-            nc.vector.tensor_copy(out=vs[:, lo : lo + n], in_=tabs[:].bitcast(U8).indirect(offs_sl(lo, n)))
+        def gather_floor(i, lo, n):
+            nc.vector.tensor_copy(out=picked(i)[:, lo : lo + n], in_=floor(i)[:].indirect(list_slice(lo, n)))
 
-        def gather_g(i, lo, n):
-            nc.vector.tensor_copy(out=gg(i)[:, lo : lo + n], in_=g(i)[:].indirect(offs_sl(lo, n)))
+        def round_w(f, a):
+            src = w_raw(f, a)[:].rearrange("p j (m t) -> p m j t", t=PACK)
+            dst = w_bf(f, a)[:].rearrange("p t m j -> p m j t")
+            cut = SCALAR_SHARE[(f, a)]
+            if cut > 0:
+                nc.scalar.activation(out=dst[:, 0:cut], in_=src[:, 0:cut], func=ACT.Copy)
+            if cut < P:
+                nc.vector.tensor_copy(out=dst[:, cut:P], in_=src[:, cut:P])
 
-        def cast_w(eng, m, a, lo, hi):
-            src = wraw(m, a)[:].rearrange("p j (m t) -> p m j t", t=4)[:, lo:hi]
-            dst = wbf(m, a)[:].rearrange("p t m j -> p m j t")[:, lo:hi]
-            if eng == "v":
-                nc.vector.tensor_copy(out=dst, in_=src)
-            elif eng == "s":
-                nc.scalar.activation(out=dst, in_=src, func=ACT.Copy)
-            else:
-                nc.gpsimd.tensor_scalar(out=dst, in0=src, scalar1=1.0, scalar2=0.0, op0=ALU.mult, op1=ALU.add)
+        def quantise_w(f, a):
+            nc.vector.quantize_mx(
+                out=w_word[f][a][:].bitcast(FP8X4),
+                scales=w_scale(f, a)[:],
+                in_=w_bf(f, a)[:].rearrange("p t m j -> p (t m j)"),
+            )
 
-        def quant_w(m, a):
-            nc.vector.quantize_mx(out=wq[m][a][:].bitcast(FP8X4), scales=wsc(m, a)[:], in_=wbf(m, a)[:].rearrange("p t m j -> p (t m j)"))
-
-        def stage1(m, b):
-            cols = slice(BLK * b, BLK * (b + 1))
-            acc = (psa, psb)[m].tile([P, 4, BLK], F32, name="acc1", tag="bank")
-            for t in range(4):
-                wcols = slice(P * t, P * (t + 1))
+        def first_product(f, b):
+            frames = slice(BLOCK * b, BLOCK * (b + 1))
+            sums = (cos_psum, sin_psum)[f].tile([P, PACK, BLOCK], F32, name="sums", tag="bank")
+            for t in range(PACK):
+                w_cols = slice(P * t, P * (t + 1))
                 for a in range(PASSES):
                     nc.tensor.matmul_mx(
-                        out=acc[:, t, :],
-                        lhsT=wq[m][a][:, wcols].bitcast(FP8X4),
-                        lhsT_scale=wsc(m, a)[:, wcols],
-                        rhs=vw(a)[:, cols].bitcast(FP8X4),
-                        rhs_scale=vs[4 * a : P, cols],
+                        out=sums[:, t, :],
+                        lhsT=w_word[f][a][:, w_cols].bitcast(FP8X4),
+                        lhsT_scale=w_scale(f, a)[:, w_cols],
+                        rhs=v_word(a)[:, frames].bitcast(FP8X4),
+                        rhs_scale=v_scale[4 * a : P, frames],
                         start=(a == 0),
                         stop=(a == PASSES - 1),
                     )
-            nc.scalar.activation(out=pbf(m, b // 4)[:, BLK * (b % 4) : BLK * (b % 4 + 1), :], in_=acc[:].rearrange("p t j -> p j t"), func=ACT.Square)
+            h, place_in_half = divmod(b, BLOCKS_PER_HALF)
+            nc.scalar.activation(
+                out=sq_bf(f, h)[:, BLOCK * place_in_half : BLOCK * (place_in_half + 1), :],
+                in_=sums[:].rearrange("p t j -> p j t"),
+                func=ACT.Square,
+            )
 
-        def warm_pe(n):
-            acc = psa.tile([P, 512], F32, name="accw", tag="bank")
-            for r in range(n):
+        def first_products(f, h):
+            for b in range(BLOCKS_PER_HALF * h, BLOCKS_PER_HALF * (h + 1)):
+                first_product(f, b)
+
+        def quantise_squares(f, h):
+            frames = slice(HALF * h, HALF * (h + 1))
+            nc.vector.quantize_mx(
+                out=sq_word[f][:, frames].bitcast(FP8X4),
+                scales=sq_scale[f][:, frames],
+                in_=sq_bf(f, h)[:].rearrange("p j t -> p (j t)"),
+            )
+
+        def second_product(h, i):
+            frames = slice(HALF * h, HALF * (h + 1))
+            power = cos_psum.tile([P, HALF], F32, name="power", tag="bank")
+            for f in (COS, SIN):
                 nc.tensor.matmul_mx(
-                    out=acc[:],
-                    lhsT=wq[0][0][:, 0:P].bitcast(FP8X4),
-                    lhsT_scale=wsc(0, 0)[:, 0:P],
-                    rhs=vw(0)[:, 0:512].bitcast(FP8X4),
-                    rhs_scale=vs[:, 0:512],
-                    start=True,
-                    stop=True,
+                    out=power[:],
+                    lhsT=wm_word[:, 2 * P * i : 2 * P * (i + 1)].bitcast(FP4X4),
+                    lhsT_scale=wm_scale[:].bitcast(U8)[:, P * i : P * (i + 1)],
+                    rhs=sq_word[f][:, frames].bitcast(FP8X4),
+                    rhs_scale=sq_scale[f][:, frames],
+                    start=(f == COS),
+                    stop=(f == SIN),
                 )
+            nc.scalar.activation(out=logs[:, i, frames], in_=power[:], func=ACT.Ln, bias=one[:, 0:1])
 
-        def quant_p(m, h):
-            cols = slice(512 * h, 512 * (h + 1))
-            nc.vector.quantize_mx(out=pq[m][:, cols].bitcast(FP8X4), scales=psc[m][:, cols], in_=pbf(m, h)[:].rearrange("p j t -> p (j t)"))
-
-        def stage2(h, i):
-            cols = slice(512 * h, 512 * (h + 1))
-            acc = psa.tile([P, 512], F32, name="acc2", tag="bank")
-            for m in range(2):
-                nc.tensor.matmul_mx(
-                    out=acc[:],
-                    lhsT=wmw[:, 2 * P * i : 2 * P * (i + 1)].bitcast(FP4X4),
-                    lhsT_scale=wms[:].bitcast(U8)[:, P * i : P * (i + 1)],
-                    rhs=pq[m][:, cols].bitcast(FP8X4),
-                    rhs_scale=psc[m][:, cols],
-                    start=(m == 0),
-                    stop=(m == 1),
-                )
-            nc.scalar.activation(out=lg[:, i, cols], in_=acc[:], func=ACT.Ln, bias=one[:, 0:1])
-
-        def sub(eng, i, lo, n):
-            e = nc.vector if eng == "v" else nc.gpsimd
-            e.tensor_tensor(out=res[:, i, lo : lo + n], in0=lg[:, i, lo : lo + n], in1=gg(i)[:, lo : lo + n], op=ALU.subtract)
-
-        def store(i, lo, n):
-            nc.sync.dma_start(out=out[P * i : P * (i + 1), lo : lo + n], in_=res[:, i, lo : lo + n])
+        def subtract_and_store(h, i):
+            frames = slice(HALF * h, HALF * (h + 1))
+            nc.vector.tensor_tensor(out=result[:, i, frames], in0=logs[:, i, frames], in1=picked(i)[:, frames], op=ALU.subtract)
+            nc.sync.dma_start(out=out[P * i : P * (i + 1), frames], in_=result[:, i, frames])
 
         nc.sync.dma_start(offsets[:], offs)
-        nc.vector.memset(tabs[:], 0)
-        nc.vector.memset(warm[:, 0:8], 1.0)
-        nc.vector.tensor_copy(out=one[:, 0:8], in_=warm[:, 0:8])
-        nc.scalar.activation(out=one[:, 8:16], in_=one[:, 0:8], func=ACT.Ln)
-        nc.vector.memset(wms[:], 0)
-        load_tab_scales_pool()
-        load_tab(0)
-        load_tab_scales_sync()
-        load_wm_words(nc.sync)
-        load_w(0, 0)
-        load_w(0, 1)
-        load_tab(1)
-        load_w(1, 0)
-        load_w(1, 1)
-        load_g(0)
-        load_wm(nc.sync)
-        load_g(1)
-        load_g(2)
+        nc.vector.memset(tab_scale[:], 0)
+        nc.vector.memset(seed[:, 0:ONES], 1.0)
+        nc.vector.tensor_copy(out=one[:, 0:ONES], in_=seed[:, 0:ONES])
+        nc.vector.memset(wm_scale[:], 0)
 
-        gather_tab(0, 0, S)
-        gather_scales(0, S)
-        cast_w("s", 0, 0, 0, 128)
-        cast_w("s", 0, 1, 0, 48)
-        cast_w("v", 0, 1, 48, 128)
-        quant_w(0, 0)
-        quant_w(0, 1)
-        warm_pe(3)
-        gather_tab(1, 0, 256)
-        gather_tab(1, 256, 256)
-        gather_tab(1, 512, 512)
-        cast_w("v", 1, 0, 0, 128)
-        quant_w(1, 0)
-        for b in range(4):
-            stage1(0, b)
-        cast_w("s", 1, 1, 0, 64)
-        cast_w("v", 1, 1, 64, 128)
-        quant_p(0, 0)
-        quant_w(1, 1)
-        for b in range(4, 8):
-            stage1(0, b)
-        quant_p(0, 1)
-        for h in range(2):
-            for b in range(4 * h, 4 * h + 4):
-                stage1(1, b)
-            quant_p(1, h)
-        for h in range(2):
-            for i in range(NT):
-                stage2(h, i)
-        gather_g(0, 0, S)
-        gather_g(1, 0, S)
-        gather_g(2, 0, 512)
-        gather_g(2, 512, 512)
-        for h in range(2):
-            for i in range(NT):
-                sub("v", i, 512 * h, 512)
-                store(i, 512 * h, 512)
+        load_tab_words(0)
+        load_tab_scales()
+        load_w(COS, 0)
+        load_w(COS, 1)
+        load_tab_words(1)
+        load_w(SIN, 0)
+        load_w(SIN, 1)
+        for i in range(BAND_TILES):
+            load_floor(i)
+        load_wm()
+
+        gather_words(0, 0, S)
+        gather_scales()
+        for a in range(PASSES):
+            round_w(COS, a)
+        for a in range(PASSES):
+            quantise_w(COS, a)
+        for lo, n in SECOND_PASS_SLICES:
+            gather_words(1, lo, n)
+
+        round_w(SIN, 0)
+        quantise_w(SIN, 0)
+        first_products(COS, 0)
+        round_w(SIN, 1)
+        quantise_squares(COS, 0)
+        quantise_w(SIN, 1)
+        first_products(COS, 1)
+
+        gather_floor(0, 0, S)
+        gather_floor(1, 0, HALF)
+        quantise_squares(COS, 1)
+        gather_floor(1, HALF, HALF)
+        for h in range(S // HALF):
+            first_products(SIN, h)
+            quantise_squares(SIN, h)
+            gather_floor(2, HALF * h, HALF)
+
+        for h in range(S // HALF):
+            for i in range(BAND_TILES):
+                second_product(h, i)
+        for h in range(S // HALF):
+            for i in range(BAND_TILES):
+                subtract_and_store(h, i)

@@ -29,24 +29,28 @@ QUADRANTS = 4
 LIST_ROWS = 16
 ONES = 8
 
-COS_BANKS, SIN_BANKS = 3, 5
+BANKS = 8
 
-SCALAR_SHARE = {(COS, 0): 128, (COS, 1): 48, (SIN, 0): 0, (SIN, 1): 64}
+SCALAR_SHARE = {(COS, 0): 128, (COS, 1): 88, (SIN, 0): 0, (SIN, 1): 88}
 
 SECOND_PASS_SLICES = ((0, 256), (256, 256), (512, 512))
 
 SEED_KIB = 66
 PLACE = {
     "seed": 0,
-    "w_raw00": 0, "w_raw01": 8, "tab_word1": 16, "w_raw10": 24, "w_raw11": 32,
-    "floor0": 40, "floor1": 48, "floor2": 56, "wm_scale": 64, "wm_word": 65,
-    "tab_word0": 66, "v_word0": 74, "w_bf00": 78, "tab_scale": 82,
-    "sq_bf00": 87, "sq_bf01": 91, "sq_bf10": 95, "sq_bf11": 99,
-    "w_scale00": 82, "w_bf01": 83,
-    "v_word1": 8, "w_bf10": 12,
-    "w_bf11": 24,
-    "picked0": 32, "picked1": 36,
-    "picked2": 95,
+    "tab_word0": 0, "w_raw01": 8, "tab_word1": 16, "floor0": 24, "w_raw10": 32, "w_raw11": 40,
+    "floor1": 48, "floor2": 56, "wm_scale": 64, "wm_word": 65,
+    "w_raw00": 66, "w_bf01": 74, "w_bf00": 78, "tab_scale": 82,
+    "w_scale00": 82, "v_word0": 82.5, "v_word1": 8,
+    "w_bf10": 74, "picked00": 32,
+    "sq_bf00": 88, "sq_bf01": 92, "sq_bf10": 96, "sq_bf11": 100,
+    "zero00": 104,
+    "w_bf11": 105, "zero01": 108.9375, "sq_scale00": 109,
+    "sq_scale01": 40, "picked10": 40.5, "picked20": 44.5,
+    "zero10": 110, "picked21": 110,
+    "zero11": 113, "logs0": 113,
+    "logs1": 119,
+    "sq_scale10": 126, "sq_scale11": 126.5,
 }
 
 
@@ -55,8 +59,7 @@ def tile_list_voiced_log_spectra_kernel(tc, tab_words, tab_scales, offs, wc, ws,
     with ExitStack() as ctx:
         keep = ctx.enter_context(tc.tile_pool(name="keep", bufs=1))
         work = ctx.enter_context(tc.tile_pool(name="work", bufs=1))
-        cos_psum = ctx.enter_context(tc.psum_pool(name="cos_psum", bufs=COS_BANKS))
-        sin_psum = ctx.enter_context(tc.psum_pool(name="sin_psum", bufs=SIN_BANKS))
+        psum = ctx.enter_context(tc.psum_pool(name="psum", bufs=BANKS))
 
         offsets = keep.tile([P, S // LIST_ROWS], U16, name="offsets")
         v_scale = keep.tile([P, S], U8, name="v_scale", align_bytes=64)
@@ -68,8 +71,7 @@ def tile_list_voiced_log_spectra_kernel(tc, tab_words, tab_scales, offs, wc, ws,
             if (f, a) != (COS, 0)
         }
         sq_word = [keep.tile([P, S], U32, name=f"sq_word{f}", align_bytes=64) for f in (COS, SIN)]
-        sq_scale = [keep.tile([P, S], U8, name=f"sq_scale{f}", align_bytes=64) for f in (COS, SIN)]
-        logs = keep.tile([P, BAND_TILES, S], F32, name="logs", align_bytes=64)
+        warm = keep.tile([P, ONES], F32, name="warm", align_bytes=64)
         result = keep.tile([P, BAND_TILES, S], F32, name="result", align_bytes=64)
         one = keep.tile([P, ONES], F32, name="one", align_bytes=64)
 
@@ -77,7 +79,7 @@ def tile_list_voiced_log_spectra_kernel(tc, tab_words, tab_scales, offs, wc, ws,
 
         def placed(name, shape, dtype):
             if name not in made:
-                made[name] = work.tile(shape, dtype, name=name, offset=1024 * PLACE[name], align_bytes=64)
+                made[name] = work.tile(shape, dtype, name=name, offset=int(1024 * PLACE[name]), align_bytes=64)
             return made[name]
 
         def tab_word(a):
@@ -96,7 +98,21 @@ def tile_list_voiced_log_spectra_kernel(tc, tab_words, tab_scales, offs, wc, ws,
             return placed(f"sq_bf{f}{h}", [P, HALF, PACK], BF16)
 
         def picked(i):
-            return placed(f"picked{i}", [P, S], F32)
+            return placed(f"picked{i}0", [P, S], F32)
+
+        def picked_half(i, h):
+            if i == 2:
+                return placed(f"picked2{h}", [P, HALF], F32)[:]
+            return picked(i)[:, HALF * h : HALF * (h + 1)]
+
+        def sq_scale(f, h):
+            return placed(f"sq_scale{f}{h}", [P, HALF], U8)
+
+        def zero(f, h):
+            return placed(f"zero{f}{h}", [P, 32], F32)
+
+        def logs(h):
+            return placed(f"logs{h}", [P, BAND_TILES, HALF], F32)
 
         def v_word(a):
             return placed(f"v_word{a}", [P, S], U32)
@@ -141,8 +157,11 @@ def tile_list_voiced_log_spectra_kernel(tc, tab_words, tab_scales, offs, wc, ws,
         def gather_scales():
             nc.vector.tensor_copy(out=v_scale[:, 0:S], in_=tab_scale[:].bitcast(U8).indirect(list_slice(0, S)))
 
-        def gather_floor(i, lo, n):
-            nc.vector.tensor_copy(out=picked(i)[:, lo : lo + n], in_=floor(i)[:].indirect(list_slice(lo, n)))
+        def gather_floor(i):
+            nc.vector.tensor_copy(out=picked(i)[:, 0:S], in_=floor(i)[:].indirect(list_slice(0, S)))
+
+        def gather_floor_half(i, h):
+            nc.vector.tensor_copy(out=picked_half(i, h), in_=floor(i)[:].indirect(list_slice(HALF * h, HALF)))
 
         def round_w(f, a):
             src = w_raw(f, a)[:].rearrange("p j (m t) -> p m j t", t=PACK)
@@ -160,106 +179,131 @@ def tile_list_voiced_log_spectra_kernel(tc, tab_words, tab_scales, offs, wc, ws,
                 in_=w_bf(f, a)[:].rearrange("p t m j -> p (t m j)"),
             )
 
-        def first_product(f, b):
+        sums = {}
+
+        def first_pass(f, b, a):
             frames = slice(BLOCK * b, BLOCK * (b + 1))
-            sums = (cos_psum, sin_psum)[f].tile([P, PACK, BLOCK], F32, name="sums", tag="bank")
+            if a == 0:
+                sums[(f, b)] = psum.tile([P, PACK, BLOCK], F32, name="sums", tag="bank")
             for t in range(PACK):
                 w_cols = slice(P * t, P * (t + 1))
-                for a in range(PASSES):
-                    nc.tensor.matmul_mx(
-                        out=sums[:, t, :],
-                        lhsT=w_word[f][a][:, w_cols].bitcast(FP8X4),
-                        lhsT_scale=w_scale(f, a)[:, w_cols],
-                        rhs=v_word(a)[:, frames].bitcast(FP8X4),
-                        rhs_scale=v_scale[4 * a : P, frames],
-                        start=(a == 0),
-                        stop=(a == PASSES - 1),
-                    )
+                nc.tensor.matmul_mx(
+                    out=sums[(f, b)][:, t, :],
+                    lhsT=w_word[f][a][:, w_cols].bitcast(FP8X4),
+                    lhsT_scale=w_scale(f, a)[:, w_cols],
+                    rhs=v_word(a)[:, frames].bitcast(FP8X4),
+                    rhs_scale=v_scale[4 * a : P, frames],
+                    start=(a == 0 and t == 0),
+                    stop=(a == PASSES - 1 and t == PACK - 1),
+                )
+
+        def square(f, b):
             h, place_in_half = divmod(b, BLOCKS_PER_HALF)
             nc.scalar.activation(
                 out=sq_bf(f, h)[:, BLOCK * place_in_half : BLOCK * (place_in_half + 1), :],
-                in_=sums[:].rearrange("p t j -> p j t"),
+                in_=sums[(f, b)][:].rearrange("p t j -> p j t"),
                 func=ACT.Square,
+                bias=zero(f, h)[:, 0:1],
             )
+
+        def open_first_products(f):
+            for b in range(BANKS):
+                first_pass(f, b, 0)
 
         def first_products(f, h):
             for b in range(BLOCKS_PER_HALF * h, BLOCKS_PER_HALF * (h + 1)):
-                first_product(f, b)
+                first_pass(f, b, 1)
+                square(f, b)
 
         def quantise_squares(f, h):
             frames = slice(HALF * h, HALF * (h + 1))
             nc.vector.quantize_mx(
                 out=sq_word[f][:, frames].bitcast(FP8X4),
-                scales=sq_scale[f][:, frames],
+                scales=sq_scale(f, h)[:],
                 in_=sq_bf(f, h)[:].rearrange("p j t -> p (j t)"),
             )
 
-        def second_product(h, i):
+        power = {}
+
+        def second_pass(h, i, f):
             frames = slice(HALF * h, HALF * (h + 1))
-            power = cos_psum.tile([P, HALF], F32, name="power", tag="bank")
-            for f in (COS, SIN):
-                nc.tensor.matmul_mx(
-                    out=power[:],
-                    lhsT=wm_word[:, 2 * P * i : 2 * P * (i + 1)].bitcast(FP4X4),
-                    lhsT_scale=wm_scale[:].bitcast(U8)[:, P * i : P * (i + 1)],
-                    rhs=sq_word[f][:, frames].bitcast(FP8X4),
-                    rhs_scale=sq_scale[f][:, frames],
-                    start=(f == COS),
-                    stop=(f == SIN),
-                )
-            nc.scalar.activation(out=logs[:, i, frames], in_=power[:], func=ACT.Ln, bias=one[:, 0:1])
+            if f == COS:
+                power[(h, i)] = psum.tile([P, HALF], F32, name="power", tag="bank")
+            nc.tensor.matmul_mx(
+                out=power[(h, i)][:],
+                lhsT=wm_word[:, 2 * P * i : 2 * P * (i + 1)].bitcast(FP4X4),
+                lhsT_scale=wm_scale[:].bitcast(U8)[:, P * i : P * (i + 1)],
+                rhs=sq_word[f][:, frames].bitcast(FP8X4),
+                rhs_scale=sq_scale(f, h)[:],
+                start=(f == COS),
+                stop=(f == SIN),
+            )
+
+        def logarithm(h, i):
+            nc.scalar.activation(out=logs(h)[:, i, :], in_=power[(h, i)][:], func=ACT.Ln, bias=one[:, 0:1])
 
         def subtract_and_store(h, i):
             frames = slice(HALF * h, HALF * (h + 1))
-            nc.vector.tensor_tensor(out=result[:, i, frames], in0=logs[:, i, frames], in1=picked(i)[:, frames], op=ALU.subtract)
+            nc.vector.tensor_tensor(out=result[:, i, frames], in0=logs(h)[:, i, :], in1=picked_half(i, h), op=ALU.subtract)
             nc.sync.dma_start(out=out[P * i : P * (i + 1), frames], in_=result[:, i, frames])
 
         nc.sync.dma_start(offsets[:], offs)
         nc.vector.memset(tab_scale[:], 0)
         nc.vector.memset(seed[:, 0:ONES], 1.0)
         nc.vector.tensor_copy(out=one[:, 0:ONES], in_=seed[:, 0:ONES])
-        nc.vector.memset(wm_scale[:], 0)
+        nc.gpsimd.memset(wm_scale[:], 0)
+        for f in (COS, SIN):
+            for h in range(S // HALF):
+                nc.gpsimd.memset(zero(f, h)[:], 0.0)
+        nc.scalar.activation(out=warm[:], in_=one[:], func=ACT.Ln)
 
-        load_tab_words(0)
-        load_tab_scales()
         load_w(COS, 0)
+        load_tab_scales()
+        load_tab_words(0)
         load_w(COS, 1)
         load_tab_words(1)
         load_w(SIN, 0)
+        load_floor(0)
         load_w(SIN, 1)
-        for i in range(BAND_TILES):
-            load_floor(i)
+        load_floor(1)
+        load_floor(2)
         load_wm()
 
-        gather_words(0, 0, S)
         gather_scales()
-        for a in range(PASSES):
-            round_w(COS, a)
-        for a in range(PASSES):
-            quantise_w(COS, a)
+        round_w(COS, 0)
+        quantise_w(COS, 0)
+        for lo, n in SECOND_PASS_SLICES:
+            gather_words(0, lo, n)
+        round_w(COS, 1)
+        open_first_products(COS)
+        quantise_w(COS, 1)
         for lo, n in SECOND_PASS_SLICES:
             gather_words(1, lo, n)
-
         round_w(SIN, 0)
         quantise_w(SIN, 0)
+        gather_floor(0)
         first_products(COS, 0)
-        round_w(SIN, 1)
-        quantise_squares(COS, 0)
-        quantise_w(SIN, 1)
         first_products(COS, 1)
-
-        gather_floor(0, 0, S)
-        gather_floor(1, 0, HALF)
+        open_first_products(SIN)
+        quantise_squares(COS, 0)
+        round_w(SIN, 1)
+        quantise_w(SIN, 1)
         quantise_squares(COS, 1)
-        gather_floor(1, HALF, HALF)
-        for h in range(S // HALF):
-            first_products(SIN, h)
-            quantise_squares(SIN, h)
-            gather_floor(2, HALF * h, HALF)
+        gather_floor(1)
+        gather_floor_half(2, 0)
+        first_products(SIN, 0)
+        quantise_squares(SIN, 0)
+        gather_floor_half(2, 1)
+        first_products(SIN, 1)
+        quantise_squares(SIN, 1)
 
         for h in range(S // HALF):
             for i in range(BAND_TILES):
-                second_product(h, i)
+                second_pass(h, i, COS)
+        for h in range(S // HALF):
+            for i in range(BAND_TILES):
+                second_pass(h, i, SIN)
+                logarithm(h, i)
         for h in range(S // HALF):
             for i in range(BAND_TILES):
                 subtract_and_store(h, i)

@@ -29,23 +29,24 @@ QUADRANTS = 4
 LIST_ROWS = 16
 ONES = 8
 
-BANKS = 8
+RING = 4
 
-SCALAR_SHARE = {(COS, 0): 128, (COS, 1): 88, (SIN, 0): 0, (SIN, 1): 88}
+SCALAR_SHARE = {(COS, 0): 128, (COS, 1): 72, (SIN, 0): 0, (SIN, 1): 64}
 
 SECOND_PASS_SLICES = ((0, 256), (256, 256), (512, 512))
 
 SEED_KIB = 66
+FIRST_PIECE = 16
 PLACE = {
     "seed": 0,
-    "tab_word0": 0, "w_raw01": 8, "tab_word1": 16, "floor0": 24, "w_raw10": 32, "w_raw11": 40,
+    "w_raw00": 0, "w_raw01": 8, "tab_word1": 16, "floor0": 24, "w_raw10": 32, "w_raw11": 40,
     "floor1": 48, "floor2": 56, "wm_scale": 64, "wm_word": 65,
-    "w_raw00": 66, "w_bf01": 74, "w_bf00": 78, "tab_scale": 82,
-    "w_scale00": 82, "v_word0": 82.5, "v_word1": 8,
-    "w_bf10": 74, "picked00": 32,
+    "tab_word0": 66, "v_word0": 74, "w_bf00": 78, "tab_scale": 82,
+    "w_scale00": 82, "w_bf01": 83, "v_word1": 8,
+    "w_bf10": 83, "picked00": 32,
     "sq_bf00": 88, "sq_bf01": 92, "sq_bf10": 96, "sq_bf11": 100,
     "zero00": 104,
-    "w_bf11": 105, "zero01": 108.9375, "sq_scale00": 109,
+    "w_bf11": 105, "zero01": 105, "zero_ws": 109, "sq_scale00": 109,
     "sq_scale01": 40, "picked10": 40.5, "picked20": 44.5,
     "zero10": 110, "picked21": 110,
     "zero11": 113, "logs0": 113,
@@ -59,7 +60,7 @@ def tile_list_voiced_log_spectra_kernel(tc, tab_words, tab_scales, offs, wc, ws,
     with ExitStack() as ctx:
         keep = ctx.enter_context(tc.tile_pool(name="keep", bufs=1))
         work = ctx.enter_context(tc.tile_pool(name="work", bufs=1))
-        psum = ctx.enter_context(tc.psum_pool(name="psum", bufs=BANKS))
+        ring = [ctx.enter_context(tc.psum_pool(name=f"ring{u}", bufs=RING)) for u in range(2)]
 
         offsets = keep.tile([P, S // LIST_ROWS], U16, name="offsets")
         v_scale = keep.tile([P, S], U8, name="v_scale", align_bytes=64)
@@ -110,6 +111,9 @@ def tile_list_voiced_log_spectra_kernel(tc, tab_words, tab_scales, offs, wc, ws,
 
         def zero(f, h):
             return placed(f"zero{f}{h}", [P, 32], F32)
+
+        def zero_ws():
+            return placed("zero_ws", [P, 32], F32)
 
         def logs(h):
             return placed(f"logs{h}", [P, BAND_TILES, HALF], F32)
@@ -167,8 +171,12 @@ def tile_list_voiced_log_spectra_kernel(tc, tab_words, tab_scales, offs, wc, ws,
             src = w_raw(f, a)[:].rearrange("p j (m t) -> p m j t", t=PACK)
             dst = w_bf(f, a)[:].rearrange("p t m j -> p m j t")
             cut = SCALAR_SHARE[(f, a)]
+            first = 0
+            if (f, a) == (SIN, 1):
+                first = FIRST_PIECE
+                nc.scalar.activation(out=dst[:, 0:first], in_=src[:, 0:first], func=ACT.Identity, bias=zero_ws()[:, 0:1])
             if cut > 0:
-                nc.scalar.activation(out=dst[:, 0:cut], in_=src[:, 0:cut], func=ACT.Copy)
+                nc.scalar.activation(out=dst[:, first:cut], in_=src[:, first:cut], func=ACT.Copy)
             if cut < P:
                 nc.vector.tensor_copy(out=dst[:, cut:P], in_=src[:, cut:P])
 
@@ -184,7 +192,7 @@ def tile_list_voiced_log_spectra_kernel(tc, tab_words, tab_scales, offs, wc, ws,
         def first_pass(f, b, a):
             frames = slice(BLOCK * b, BLOCK * (b + 1))
             if a == 0:
-                sums[(f, b)] = psum.tile([P, PACK, BLOCK], F32, name="sums", tag="bank")
+                sums[(f, b)] = ring[1 if (f == SIN and b < RING) else 0].tile([P, PACK, BLOCK], F32, name="sums", tag="bank")
             for t in range(PACK):
                 w_cols = slice(P * t, P * (t + 1))
                 nc.tensor.matmul_mx(
@@ -207,13 +215,15 @@ def tile_list_voiced_log_spectra_kernel(tc, tab_words, tab_scales, offs, wc, ws,
             )
 
         def open_first_products(f):
-            for b in range(BANKS):
+            for b in range(RING if f == COS else 2 * RING):
                 first_pass(f, b, 0)
 
         def first_products(f, h):
             for b in range(BLOCKS_PER_HALF * h, BLOCKS_PER_HALF * (h + 1)):
                 first_pass(f, b, 1)
                 square(f, b)
+                if f == COS and b < RING:
+                    first_pass(f, b + RING, 0)
 
         def quantise_squares(f, h):
             frames = slice(HALF * h, HALF * (h + 1))
@@ -228,7 +238,7 @@ def tile_list_voiced_log_spectra_kernel(tc, tab_words, tab_scales, offs, wc, ws,
         def second_pass(h, i, f):
             frames = slice(HALF * h, HALF * (h + 1))
             if f == COS:
-                power[(h, i)] = psum.tile([P, HALF], F32, name="power", tag="bank")
+                power[(h, i)] = ring[1 - h].tile([P, HALF], F32, name="power", tag="bank")
             nc.tensor.matmul_mx(
                 out=power[(h, i)][:],
                 lhsT=wm_word[:, 2 * P * i : 2 * P * (i + 1)].bitcast(FP4X4),
@@ -242,9 +252,10 @@ def tile_list_voiced_log_spectra_kernel(tc, tab_words, tab_scales, offs, wc, ws,
         def logarithm(h, i):
             nc.scalar.activation(out=logs(h)[:, i, :], in_=power[(h, i)][:], func=ACT.Ln, bias=one[:, 0:1])
 
-        def subtract_and_store(h, i):
-            frames = slice(HALF * h, HALF * (h + 1))
-            nc.vector.tensor_tensor(out=result[:, i, frames], in0=logs(h)[:, i, :], in1=picked_half(i, h), op=ALU.subtract)
+        def subtract_and_store(h, i, lo, n):
+            part = slice(lo, lo + n)
+            frames = slice(HALF * h + lo, HALF * h + lo + n)
+            nc.vector.tensor_tensor(out=result[:, i, frames], in0=logs(h)[:, i, part], in1=picked_half(i, h)[:, part], op=ALU.subtract)
             nc.sync.dma_start(out=out[P * i : P * (i + 1), frames], in_=result[:, i, frames])
 
         nc.sync.dma_start(offsets[:], offs)
@@ -255,11 +266,12 @@ def tile_list_voiced_log_spectra_kernel(tc, tab_words, tab_scales, offs, wc, ws,
         for f in (COS, SIN):
             for h in range(S // HALF):
                 nc.gpsimd.memset(zero(f, h)[:], 0.0)
+        nc.gpsimd.memset(zero_ws()[:], 0.0)
         nc.scalar.activation(out=warm[:], in_=one[:], func=ACT.Ln)
 
-        load_w(COS, 0)
-        load_tab_scales()
         load_tab_words(0)
+        load_tab_scales()
+        load_w(COS, 0)
         load_w(COS, 1)
         load_tab_words(1)
         load_w(SIN, 0)
@@ -269,12 +281,11 @@ def tile_list_voiced_log_spectra_kernel(tc, tab_words, tab_scales, offs, wc, ws,
         load_floor(2)
         load_wm()
 
+        gather_words(0, 0, S)
         gather_scales()
         round_w(COS, 0)
-        quantise_w(COS, 0)
-        for lo, n in SECOND_PASS_SLICES:
-            gather_words(0, lo, n)
         round_w(COS, 1)
+        quantise_w(COS, 0)
         open_first_products(COS)
         quantise_w(COS, 1)
         for lo, n in SECOND_PASS_SLICES:
@@ -285,8 +296,8 @@ def tile_list_voiced_log_spectra_kernel(tc, tab_words, tab_scales, offs, wc, ws,
         first_products(COS, 0)
         first_products(COS, 1)
         open_first_products(SIN)
-        quantise_squares(COS, 0)
         round_w(SIN, 1)
+        quantise_squares(COS, 0)
         quantise_w(SIN, 1)
         quantise_squares(COS, 1)
         gather_floor(1)
@@ -300,10 +311,11 @@ def tile_list_voiced_log_spectra_kernel(tc, tab_words, tab_scales, offs, wc, ws,
         for h in range(S // HALF):
             for i in range(BAND_TILES):
                 second_pass(h, i, COS)
-        for h in range(S // HALF):
             for i in range(BAND_TILES):
                 second_pass(h, i, SIN)
                 logarithm(h, i)
         for h in range(S // HALF):
             for i in range(BAND_TILES):
-                subtract_and_store(h, i)
+                pieces = 2 if (h, i) == (1, BAND_TILES - 1) else 1
+                for u in range(pieces):
+                    subtract_and_store(h, i, u * HALF // pieces, HALF // pieces)

@@ -31,27 +31,28 @@ ONES = 8
 
 RING = 4
 
-SCALAR_SHARE = {(COS, 0): 128, (COS, 1): 72, (SIN, 0): 0, (SIN, 1): 64}
+SCALAR_SHARE = {(COS, 0): 128, (COS, 1): 72, (SIN, 0): 0, (SIN, 1): 0}
 
 SECOND_PASS_SLICES = ((0, 256), (256, 256), (512, 512))
 
 SEED_KIB = 66
-FIRST_PIECE = 16
+FIRST_PIECE = 32
 PLACE = {
     "seed": 0,
     "w_raw00": 0, "w_raw01": 8, "tab_word1": 16, "floor0": 24, "w_raw10": 32, "w_raw11": 40,
     "floor1": 48, "floor2": 56, "wm_scale": 64, "wm_word": 65,
     "tab_word0": 66, "v_word0": 74, "w_bf00": 78, "tab_scale": 82,
     "w_scale00": 82, "w_bf01": 83, "v_word1": 8,
-    "w_bf10": 83, "picked00": 32,
+    "w_bf10": 83,
     "sq_bf00": 88, "sq_bf01": 92, "sq_bf10": 96, "sq_bf11": 100,
-    "zero00": 104,
-    "w_bf11": 105, "zero01": 105, "zero_ws": 109, "sq_scale00": 109,
-    "sq_scale01": 40, "picked10": 40.5, "picked20": 44.5,
-    "zero10": 110, "picked21": 110,
-    "zero11": 113, "logs0": 113,
-    "logs1": 119,
-    "sq_scale10": 126, "sq_scale11": 126.5,
+    "zero00": 128, "w_bf11": 32,
+    "zero01": 104, "sq_scale00": 44,
+    "picked00": 40,
+    "sq_scale01": 106, "zero_first": 106.4375, "picked10": 106.5,
+    "zero10": 109, "picked11": 109,
+    "picked20": 111, "zero11": 114.9375, "logs0": 115,
+    "logs1": 121,
+    "sq_scale10": 127, "sq_scale11": 127.5,
 }
 
 
@@ -102,8 +103,8 @@ def tile_list_voiced_log_spectra_kernel(tc, tab_words, tab_scales, offs, wc, ws,
             return placed(f"picked{i}0", [P, S], F32)
 
         def picked_half(i, h):
-            if i == 2:
-                return placed(f"picked2{h}", [P, HALF], F32)[:]
+            if i == 1:
+                return placed(f"picked1{h}", [P, HALF], F32)[:]
             return picked(i)[:, HALF * h : HALF * (h + 1)]
 
         def sq_scale(f, h):
@@ -114,6 +115,9 @@ def tile_list_voiced_log_spectra_kernel(tc, tab_words, tab_scales, offs, wc, ws,
 
         def zero_ws():
             return placed("zero_ws", [P, 32], F32)
+
+        def zero_first():
+            return placed("zero_first", [P, 32], F32)
 
         def logs(h):
             return placed(f"logs{h}", [P, BAND_TILES, HALF], F32)
@@ -171,12 +175,8 @@ def tile_list_voiced_log_spectra_kernel(tc, tab_words, tab_scales, offs, wc, ws,
             src = w_raw(f, a)[:].rearrange("p j (m t) -> p m j t", t=PACK)
             dst = w_bf(f, a)[:].rearrange("p t m j -> p m j t")
             cut = SCALAR_SHARE[(f, a)]
-            first = 0
-            if (f, a) == (SIN, 1):
-                first = FIRST_PIECE
-                nc.scalar.activation(out=dst[:, 0:first], in_=src[:, 0:first], func=ACT.Identity, bias=zero_ws()[:, 0:1])
             if cut > 0:
-                nc.scalar.activation(out=dst[:, first:cut], in_=src[:, first:cut], func=ACT.Copy)
+                nc.scalar.activation(out=dst[:, 0:cut], in_=src[:, 0:cut], func=ACT.Copy)
             if cut < P:
                 nc.vector.tensor_copy(out=dst[:, cut:P], in_=src[:, cut:P])
 
@@ -211,7 +211,7 @@ def tile_list_voiced_log_spectra_kernel(tc, tab_words, tab_scales, offs, wc, ws,
                 out=sq_bf(f, h)[:, BLOCK * place_in_half : BLOCK * (place_in_half + 1), :],
                 in_=sums[(f, b)][:].rearrange("p t j -> p j t"),
                 func=ACT.Square,
-                bias=zero(f, h)[:, 0:1],
+                bias=(zero_first() if (f, b) == (SIN, 0) else zero(f, h))[:, 0:1],
             )
 
         def open_first_products(f):
@@ -255,7 +255,8 @@ def tile_list_voiced_log_spectra_kernel(tc, tab_words, tab_scales, offs, wc, ws,
         def subtract_and_store(h, i, lo, n):
             part = slice(lo, lo + n)
             frames = slice(HALF * h + lo, HALF * h + lo + n)
-            nc.vector.tensor_tensor(out=result[:, i, frames], in0=logs(h)[:, i, part], in1=picked_half(i, h)[:, part], op=ALU.subtract)
+            engine = nc.gpsimd if (h == 0 and i < 2) else nc.vector
+            engine.tensor_tensor(out=result[:, i, frames], in0=logs(h)[:, i, part], in1=picked_half(i, h)[:, part], op=ALU.subtract)
             nc.sync.dma_start(out=out[P * i : P * (i + 1), frames], in_=result[:, i, frames])
 
         nc.sync.dma_start(offsets[:], offs)
@@ -266,7 +267,7 @@ def tile_list_voiced_log_spectra_kernel(tc, tab_words, tab_scales, offs, wc, ws,
         for f in (COS, SIN):
             for h in range(S // HALF):
                 nc.gpsimd.memset(zero(f, h)[:], 0.0)
-        nc.gpsimd.memset(zero_ws()[:], 0.0)
+        nc.gpsimd.memset(zero_first()[:], 0.0)
         nc.scalar.activation(out=warm[:], in_=one[:], func=ACT.Ln)
 
         load_tab_words(0)
@@ -275,11 +276,11 @@ def tile_list_voiced_log_spectra_kernel(tc, tab_words, tab_scales, offs, wc, ws,
         load_w(COS, 1)
         load_tab_words(1)
         load_w(SIN, 0)
-        load_floor(0)
         load_w(SIN, 1)
+        load_floor(0)
         load_floor(1)
-        load_floor(2)
         load_wm()
+        load_floor(2)
 
         gather_words(0, 0, S)
         gather_scales()
@@ -292,21 +293,22 @@ def tile_list_voiced_log_spectra_kernel(tc, tab_words, tab_scales, offs, wc, ws,
             gather_words(1, lo, n)
         round_w(SIN, 0)
         quantise_w(SIN, 0)
-        gather_floor(0)
         first_products(COS, 0)
+        round_w(SIN, 1)
+        quantise_w(SIN, 1)
+        quantise_squares(COS, 0)
+        gather_floor(0)
         first_products(COS, 1)
         open_first_products(SIN)
-        round_w(SIN, 1)
-        quantise_squares(COS, 0)
-        quantise_w(SIN, 1)
-        quantise_squares(COS, 1)
-        gather_floor(1)
-        gather_floor_half(2, 0)
         first_products(SIN, 0)
+        quantise_squares(COS, 1)
+        gather_floor_half(1, 0)
         quantise_squares(SIN, 0)
-        gather_floor_half(2, 1)
+        gather_floor_half(1, 1)
         first_products(SIN, 1)
         quantise_squares(SIN, 1)
+        for h in range(S // HALF):
+            gather_floor_half(2, h)
 
         for h in range(S // HALF):
             for i in range(BAND_TILES):

@@ -29,13 +29,16 @@ QUADRANTS = 4
 LIST_ROWS = 16
 ONES = 8
 
-RING = 4
+SUM_BANK = ((0, 1, 2, 3, 0, 1, 2, 3), (4, 5, 6, 7, 0, 1, 4, 5))
+POWER_BANK = ((2, 3, 6), (0, 7, 1))
+AHEAD = (4, 6)
 
-SCALAR_SHARE = {(COS, 0): 128, (COS, 1): 72, (SIN, 0): 0, (SIN, 1): 0}
+SCALAR_SHARE = {(COS, 0): 128, (COS, 1): 72, (SIN, 0): 0, (SIN, 1): 40}
 
 SECOND_PASS_SLICES = ((0, 256), (256, 256), (512, 512))
 
 SEED_KIB = 66
+CUT = 768
 FIRST_PIECE = 32
 PLACE = {
     "seed": 0,
@@ -44,12 +47,12 @@ PLACE = {
     "tab_word0": 66, "v_word0": 74, "w_bf00": 78, "tab_scale": 82,
     "w_scale00": 82, "w_bf01": 83, "v_word1": 8,
     "w_bf10": 83,
-    "sq_bf00": 88, "sq_bf01": 92, "sq_bf10": 96, "sq_bf11": 100,
-    "zero00": 128, "w_bf11": 32,
-    "zero01": 104, "sq_scale00": 44,
+    "sq_bf00": 87, "sq_bf01": 92, "sq_bf10": 96, "sq_bf11": 100,
+    "zero00": 128, "w_bf11": 128,
+    "zero01": 104, "sq_scale00": 91.5, "zero_ws": 91.9375,
     "picked00": 40,
-    "sq_scale01": 106, "zero_first": 106.4375, "picked10": 106.5,
-    "zero10": 109, "picked11": 109,
+    "picked11": 105, "zero_first": 105.9375, "sq_scale01": 106,
+    "zero10": 107, "picked10": 107,
     "picked20": 111, "zero11": 114.9375, "logs0": 115,
     "logs1": 121,
     "sq_scale10": 127, "sq_scale11": 127.5,
@@ -61,7 +64,7 @@ def tile_list_voiced_log_spectra_kernel(tc, tab_words, tab_scales, offs, wc, ws,
     with ExitStack() as ctx:
         keep = ctx.enter_context(tc.tile_pool(name="keep", bufs=1))
         work = ctx.enter_context(tc.tile_pool(name="work", bufs=1))
-        ring = [ctx.enter_context(tc.psum_pool(name=f"ring{u}", bufs=RING)) for u in range(2)]
+        psum = ctx.enter_context(tc.psum_pool(name="psum", bufs=1))
 
         offsets = keep.tile([P, S // LIST_ROWS], U16, name="offsets")
         v_scale = keep.tile([P, S], U8, name="v_scale", align_bytes=64)
@@ -102,10 +105,12 @@ def tile_list_voiced_log_spectra_kernel(tc, tab_words, tab_scales, offs, wc, ws,
         def picked(i):
             return placed(f"picked{i}0", [P, S], F32)
 
-        def picked_half(i, h):
+        def picked_part(i, lo, n):
+            if i == 1 and lo < CUT:
+                return placed("picked10", [P, CUT], F32)[:, lo : lo + n]
             if i == 1:
-                return placed(f"picked1{h}", [P, HALF], F32)[:]
-            return picked(i)[:, HALF * h : HALF * (h + 1)]
+                return placed("picked11", [P, S - CUT], F32)[:, lo - CUT : lo - CUT + n]
+            return picked(i)[:, lo : lo + n]
 
         def sq_scale(f, h):
             return placed(f"sq_scale{f}{h}", [P, HALF], U8)
@@ -165,17 +170,16 @@ def tile_list_voiced_log_spectra_kernel(tc, tab_words, tab_scales, offs, wc, ws,
         def gather_scales():
             nc.vector.tensor_copy(out=v_scale[:, 0:S], in_=tab_scale[:].bitcast(U8).indirect(list_slice(0, S)))
 
-        def gather_floor(i):
-            nc.vector.tensor_copy(out=picked(i)[:, 0:S], in_=floor(i)[:].indirect(list_slice(0, S)))
-
-        def gather_floor_half(i, h):
-            nc.vector.tensor_copy(out=picked_half(i, h), in_=floor(i)[:].indirect(list_slice(HALF * h, HALF)))
+        def gather_floor(i, lo, n):
+            nc.vector.tensor_copy(out=picked_part(i, lo, n), in_=floor(i)[:].indirect(list_slice(lo, n)))
 
         def round_w(f, a):
             src = w_raw(f, a)[:].rearrange("p j (m t) -> p m j t", t=PACK)
             dst = w_bf(f, a)[:].rearrange("p t m j -> p m j t")
             cut = SCALAR_SHARE[(f, a)]
-            if cut > 0:
+            if (f, a) == (SIN, 1):
+                nc.scalar.activation(out=dst[:, 0:cut], in_=src[:, 0:cut], func=ACT.Identity, bias=zero_ws()[:, 0:1])
+            elif cut > 0:
                 nc.scalar.activation(out=dst[:, 0:cut], in_=src[:, 0:cut], func=ACT.Copy)
             if cut < P:
                 nc.vector.tensor_copy(out=dst[:, cut:P], in_=src[:, cut:P])
@@ -192,7 +196,7 @@ def tile_list_voiced_log_spectra_kernel(tc, tab_words, tab_scales, offs, wc, ws,
         def first_pass(f, b, a):
             frames = slice(BLOCK * b, BLOCK * (b + 1))
             if a == 0:
-                sums[(f, b)] = ring[1 if (f == SIN and b < RING) else 0].tile([P, PACK, BLOCK], F32, name="sums", tag="bank")
+                sums[(f, b)] = psum.tile([P, PACK, BLOCK], F32, name="sums", tag=f"bank{SUM_BANK[f][b]}")
             for t in range(PACK):
                 w_cols = slice(P * t, P * (t + 1))
                 nc.tensor.matmul_mx(
@@ -215,15 +219,15 @@ def tile_list_voiced_log_spectra_kernel(tc, tab_words, tab_scales, offs, wc, ws,
             )
 
         def open_first_products(f):
-            for b in range(RING if f == COS else 2 * RING):
+            for b in range(AHEAD[f]):
                 first_pass(f, b, 0)
 
         def first_products(f, h):
             for b in range(BLOCKS_PER_HALF * h, BLOCKS_PER_HALF * (h + 1)):
                 first_pass(f, b, 1)
                 square(f, b)
-                if f == COS and b < RING:
-                    first_pass(f, b + RING, 0)
+                if b + AHEAD[f] < S // BLOCK:
+                    first_pass(f, b + AHEAD[f], 0)
 
         def quantise_squares(f, h):
             frames = slice(HALF * h, HALF * (h + 1))
@@ -237,26 +241,25 @@ def tile_list_voiced_log_spectra_kernel(tc, tab_words, tab_scales, offs, wc, ws,
 
         def second_pass(h, i, f):
             frames = slice(HALF * h, HALF * (h + 1))
-            if f == COS:
-                power[(h, i)] = ring[1 - h].tile([P, HALF], F32, name="power", tag="bank")
+            if f == SIN - h:
+                power[(h, i)] = psum.tile([P, HALF], F32, name="power", tag=f"bank{POWER_BANK[h][i]}")
             nc.tensor.matmul_mx(
                 out=power[(h, i)][:],
                 lhsT=wm_word[:, 2 * P * i : 2 * P * (i + 1)].bitcast(FP4X4),
                 lhsT_scale=wm_scale[:].bitcast(U8)[:, P * i : P * (i + 1)],
                 rhs=sq_word[f][:, frames].bitcast(FP8X4),
                 rhs_scale=sq_scale(f, h)[:],
-                start=(f == COS),
-                stop=(f == SIN),
+                start=(f == SIN - h),
+                stop=(f == h),
             )
 
         def logarithm(h, i):
             nc.scalar.activation(out=logs(h)[:, i, :], in_=power[(h, i)][:], func=ACT.Ln, bias=one[:, 0:1])
 
-        def subtract_and_store(h, i, lo, n):
+        def subtract_and_store(engine, h, i, lo, n):
             part = slice(lo, lo + n)
             frames = slice(HALF * h + lo, HALF * h + lo + n)
-            engine = nc.gpsimd if (h == 0 and i < 2) else nc.vector
-            engine.tensor_tensor(out=result[:, i, frames], in0=logs(h)[:, i, part], in1=picked_half(i, h)[:, part], op=ALU.subtract)
+            engine.tensor_tensor(out=result[:, i, frames], in0=logs(h)[:, i, part], in1=picked_part(i, HALF * h + lo, n), op=ALU.subtract)
             nc.sync.dma_start(out=out[P * i : P * (i + 1), frames], in_=result[:, i, frames])
 
         nc.sync.dma_start(offsets[:], offs)
@@ -266,8 +269,9 @@ def tile_list_voiced_log_spectra_kernel(tc, tab_words, tab_scales, offs, wc, ws,
         nc.gpsimd.memset(wm_scale[:], 0)
         for f in (COS, SIN):
             for h in range(S // HALF):
-                nc.gpsimd.memset(zero(f, h)[:], 0.0)
+                nc.gpsimd.memset(zero(f, h)[:, 0:ONES], 0.0)
         nc.gpsimd.memset(zero_first()[:], 0.0)
+        nc.gpsimd.memset(zero_ws()[:], 0.0)
         nc.scalar.activation(out=warm[:], in_=one[:], func=ACT.Ln)
 
         load_tab_words(0)
@@ -295,29 +299,34 @@ def tile_list_voiced_log_spectra_kernel(tc, tab_words, tab_scales, offs, wc, ws,
         quantise_w(SIN, 0)
         first_products(COS, 0)
         round_w(SIN, 1)
-        quantise_w(SIN, 1)
         quantise_squares(COS, 0)
-        gather_floor(0)
+        quantise_w(SIN, 1)
+        gather_floor(0, 0, S)
         first_products(COS, 1)
         open_first_products(SIN)
         first_products(SIN, 0)
         quantise_squares(COS, 1)
-        gather_floor_half(1, 0)
+        gather_floor(1, CUT, S - CUT)
         quantise_squares(SIN, 0)
-        gather_floor_half(1, 1)
+        gather_floor(1, 0, CUT)
         first_products(SIN, 1)
         quantise_squares(SIN, 1)
         for h in range(S // HALF):
-            gather_floor_half(2, h)
+            gather_floor(2, HALF * h, HALF)
 
-        for h in range(S // HALF):
-            for i in range(BAND_TILES):
-                second_pass(h, i, COS)
-            for i in range(BAND_TILES):
-                second_pass(h, i, SIN)
-                logarithm(h, i)
-        for h in range(S // HALF):
-            for i in range(BAND_TILES):
-                pieces = 2 if (h, i) == (1, BAND_TILES - 1) else 1
-                for u in range(pieces):
-                    subtract_and_store(h, i, u * HALF // pieces, HALF // pieces)
+        for i in range(BAND_TILES):
+            second_pass(0, i, SIN)
+            second_pass(0, i, COS)
+            logarithm(0, i)
+        for i in (1, 0, 2):
+            second_pass(1, i, COS)
+        for i in (1, 0, 2):
+            second_pass(1, i, SIN)
+            logarithm(1, i)
+        subtract_and_store(nc.gpsimd, 0, 0, 0, HALF)
+        subtract_and_store(nc.gpsimd, 0, 1, 0, HALF)
+        subtract_and_store(nc.gpsimd, 1, 1, 0, 256)
+        subtract_and_store(nc.vector, 0, 2, 0, HALF)
+        subtract_and_store(nc.vector, 1, 0, 0, HALF)
+        subtract_and_store(nc.vector, 1, 2, 0, HALF)
+        subtract_and_store(nc.vector, 1, 1, 256, 256)

@@ -325,8 +325,8 @@ def tile_list_voiced_log_spectra_kernel(tc, tab_words, tab_scales, offs, wc, ws,
             logarithm(1, i)
         subtract_and_store(nc.gpsimd, 0, 0, 0, HALF)
         subtract_and_store(nc.gpsimd, 0, 1, 0, HALF)
-        subtract_and_store(nc.gpsimd, 1, 1, 0, 256)
         subtract_and_store(nc.vector, 0, 2, 0, HALF)
+        subtract_and_store(nc.vector, 1, 1, 0, 256)
         subtract_and_store(nc.vector, 1, 0, 0, HALF)
         subtract_and_store(nc.vector, 1, 2, 0, HALF)
         subtract_and_store(nc.vector, 1, 1, 256, 256)

@@ -33,24 +33,23 @@ SUM_BANK = ((0, 1, 2, 3, 0, 1, 2, 3), (4, 5, 6, 7, 0, 1, 4, 5))
 POWER_BANK = ((2, 3, 6), (0, 7, 1))
 AHEAD = (4, 6)
 
-SCALAR_SHARE = {(COS, 0): 128, (COS, 1): 72, (SIN, 0): 0, (SIN, 1): 40}
+SCALAR_SHARE = {(COS, 0): 88, (COS, 1): 72, (SIN, 0): 0, (SIN, 1): 40}
 
 SECOND_PASS_SLICES = ((0, 256), (256, 256), (512, 512))
 
-SEED_KIB = 66
+SEED_KIB = 52
 CUT = 768
 FIRST_PIECE = 32
 PLACE = {
-    "seed": 0,
-    "w_raw00": 0, "w_raw01": 8, "tab_word1": 16, "floor0": 24, "w_raw10": 32, "w_raw11": 40,
-    "floor1": 48, "floor2": 56, "wm_scale": 64, "wm_word": 65,
-    "tab_word0": 66, "v_word0": 74, "w_bf00": 78, "tab_scale": 82,
+    "w_raw00": 0, "w_raw01": 8, "flat": 16, "seed": 16, "tab_word1": 18, "floor0": 26, "w_raw10": 34, "w_raw11": 42,
+    "floor1": 50, "floor2": 58, "wm_scale": 66, "wm_word": 67,
+    "tab_word0": 136, "v_word0": 74, "w_bf00": 78,
     "w_scale00": 82, "w_bf01": 83, "v_word1": 8,
     "w_bf10": 83,
     "sq_bf00": 87, "sq_bf01": 92, "sq_bf10": 96, "sq_bf11": 100,
     "zero00": 128, "w_bf11": 128,
     "zero01": 104, "sq_scale00": 91.5, "zero_ws": 91.9375,
-    "picked00": 40,
+    "picked00": 42,
     "picked11": 105, "zero_first": 105.9375, "sq_scale01": 106,
     "zero10": 107, "picked10": 107,
     "picked20": 111, "zero11": 114.9375, "logs0": 115,
@@ -67,7 +66,7 @@ def tile_list_voiced_log_spectra_kernel(tc, tab_words, tab_scales, offs, wc, ws,
         psum = ctx.enter_context(tc.psum_pool(name="psum", bufs=1))
 
         offsets = keep.tile([P, S // LIST_ROWS], U16, name="offsets")
-        v_scale = keep.tile([P, S], U8, name="v_scale", align_bytes=64)
+        v_scale = [keep.tile([P, S], U8, name=f"v_scale{a}", align_bytes=64) for a in range(PASSES)]
         w_word = [[keep.tile([P, H], U32, name=f"w_word{f}{a}", align_bytes=64) for a in range(PASSES)] for f in (COS, SIN)]
         w_scale_kept = {
             (f, a): keep.tile([P, H], U8, name=f"w_scale{f}{a}", align_bytes=64)
@@ -78,6 +77,7 @@ def tile_list_voiced_log_spectra_kernel(tc, tab_words, tab_scales, offs, wc, ws,
         sq_word = [keep.tile([P, S], U32, name=f"sq_word{f}", align_bytes=64) for f in (COS, SIN)]
         warm = keep.tile([P, ONES], F32, name="warm", align_bytes=64)
         result = keep.tile([P, BAND_TILES, S], F32, name="result", align_bytes=64)
+        warm_in = keep.tile([P, ONES], F32, name="warm_in", align_bytes=64)
         one = keep.tile([P, ONES], F32, name="one", align_bytes=64)
 
         made = {}
@@ -133,10 +133,8 @@ def tile_list_voiced_log_spectra_kernel(tc, tab_words, tab_scales, offs, wc, ws,
         def w_scale(f, a):
             return placed("w_scale00", [P, H], U8) if (f, a) == (COS, 0) else w_scale_kept[(f, a)]
 
-        tab_scale = placed("tab_scale", [P, T // 4], I32)
-        seed = placed("seed", [P, SEED_KIB * 256], F32)
-        wm_word = placed("wm_word", [P, 2 * N], U8)
-        wm_scale = placed("wm_scale", [P, N // 4], I32)
+        tab_scale = placed("flat", [P, T // 4], I32)
+        flat_picked = keep.tile([P, S], U8, name="flat_picked", align_bytes=64)
 
         def load_tab_words(a):
             nc.sync.dma_start(out=tab_word(a)[:], in_=tab_words[a].rearrange("p t i -> p (t i)").bitcast(I32))
@@ -149,12 +147,15 @@ def tile_list_voiced_log_spectra_kernel(tc, tab_words, tab_scales, offs, wc, ws,
             nc.sync.dma_start(out=floor(i)[:], in_=gT[P * i : P * (i + 1), :])
 
         def load_tab_scales():
-            for q in range(QUADRANTS // 2):
-                nc.sync.dma_start(out=tab_scale[32 * q : 32 * q + 8, :], in_=tab_scales[:, 4 * q : 4 * q + 4, :].bitcast(I32))
-            for q in range(QUADRANTS // 2, QUADRANTS):
-                for a in range(PASSES):
-                    rows = slice(32 * q + 4 * a, 32 * q + 4 * a + 4)
-                    nc.sync.dma_start(out=tab_scale[rows, :], in_=tab_scales[a, 4 * q : 4 * q + 4, :].bitcast(I32))
+            nc.sync.dma_start(out=tab_scale[0:32, :], in_=tab_scales.rearrange("a q t -> (a q) t").bitcast(I32))
+
+        def move_scales(a, q):
+            src = flat_picked[16 * a + 4 * q : 16 * a + 4 * q + 4, :].bitcast(I32)
+            dst = v_scale[a][32 * q + 4 * a : 32 * q + 4 * a + 4, :].bitcast(I32)
+            if (a, q) == (0, 0):
+                nc.vector.tensor_copy(out=dst, in_=src)
+            else:
+                nc.sync.dma_start(out=dst, in_=src)
 
         def load_wm():
             nc.sync.dma_start(out=wm_word[:].bitcast(I32), in_=wm_words[0].bitcast(I32))
@@ -168,7 +169,7 @@ def tile_list_voiced_log_spectra_kernel(tc, tab_words, tab_scales, offs, wc, ws,
             nc.vector.tensor_copy(out=v_word(a)[:, lo : lo + n], in_=tab_word(a)[:].bitcast(U32).indirect(list_slice(lo, n)))
 
         def gather_scales():
-            nc.vector.tensor_copy(out=v_scale[:, 0:S], in_=tab_scale[:].bitcast(U8).indirect(list_slice(0, S)))
+            nc.vector.tensor_copy(out=flat_picked[:], in_=tab_scale[:].bitcast(U8).indirect(list_slice(0, S)))
 
         def gather_floor(i, lo, n):
             nc.vector.tensor_copy(out=picked_part(i, lo, n), in_=floor(i)[:].indirect(list_slice(lo, n)))
@@ -204,7 +205,7 @@ def tile_list_voiced_log_spectra_kernel(tc, tab_words, tab_scales, offs, wc, ws,
                     lhsT=w_word[f][a][:, w_cols].bitcast(FP8X4),
                     lhsT_scale=w_scale(f, a)[:, w_cols],
                     rhs=v_word(a)[:, frames].bitcast(FP8X4),
-                    rhs_scale=v_scale[4 * a : P, frames],
+                    rhs_scale=v_scale[a][4 * a : P, frames],
                     start=(a == 0 and t == 0),
                     stop=(a == PASSES - 1 and t == PACK - 1),
                 )
@@ -263,22 +264,34 @@ def tile_list_voiced_log_spectra_kernel(tc, tab_words, tab_scales, offs, wc, ws,
             nc.sync.dma_start(out=out[P * i : P * (i + 1), frames], in_=result[:, i, frames])
 
         nc.sync.dma_start(offsets[:], offs)
-        nc.vector.memset(tab_scale[:], 0)
-        nc.vector.memset(seed[:, 0:ONES], 1.0)
-        nc.vector.tensor_copy(out=one[:, 0:ONES], in_=seed[:, 0:ONES])
-        nc.gpsimd.memset(wm_scale[:], 0)
+        nc.vector.memset(tab_scale[32:64, :], 0)
+        nc.vector.memset(tab_scale[64:P, :], 0)
+        nc.vector.memset(warm_in[:], 1.0)
+        for a in range(PASSES):
+            nc.vector.memset(v_scale[a][:].bitcast(I32), 0)
         for f in (COS, SIN):
             for h in range(S // HALF):
                 nc.gpsimd.memset(zero(f, h)[:, 0:ONES], 0.0)
         nc.gpsimd.memset(zero_first()[:], 0.0)
         nc.gpsimd.memset(zero_ws()[:], 0.0)
-        nc.scalar.activation(out=warm[:], in_=one[:], func=ACT.Ln)
+        nc.scalar.activation(out=warm[:], in_=warm_in[:], func=ACT.Ln)
 
-        load_tab_words(0)
         load_tab_scales()
+        load_tab_words(0)
         load_w(COS, 0)
         load_w(COS, 1)
+        gather_scales()
+        seed = placed("seed", [P, SEED_KIB * 256], F32)
+        nc.gpsimd.memset(seed[:, 0:ONES], 1.0)
+        nc.gpsimd.tensor_copy(out=one[:], in_=seed[:, 0:ONES])
+        wm_word = placed("wm_word", [P, 2 * N], U8)
+        wm_scale = placed("wm_scale", [P, N // 4], I32)
+        nc.gpsimd.memset(wm_scale[:], 0)
+        moves = [(a, q) for a in range(PASSES) for q in range(QUADRANTS)]
+        for a, q in moves[1:7]:
+            move_scales(a, q)
         load_tab_words(1)
+        move_scales(*moves[7])
         load_w(SIN, 0)
         load_w(SIN, 1)
         load_floor(0)
@@ -287,7 +300,7 @@ def tile_list_voiced_log_spectra_kernel(tc, tab_words, tab_scales, offs, wc, ws,
         load_floor(2)
 
         gather_words(0, 0, S)
-        gather_scales()
+        move_scales(*moves[0])
         round_w(COS, 0)
         round_w(COS, 1)
         quantise_w(COS, 0)

@@ -29,32 +29,34 @@ QUADRANTS = 4
 LIST_ROWS = 16
 ONES = 8
 
+QUARTER = 256
 SUM_BANK = ((0, 1, 2, 3, 0, 1, 2, 3), (4, 5, 6, 7, 0, 1, 4, 5))
-POWER_BANK = ((2, 3, 6), (0, 7, 1))
 AHEAD = (4, 6)
-
 SCALAR_SHARE = {(COS, 0): 88, (COS, 1): 72, (SIN, 0): 0, (SIN, 1): 40}
-
 SECOND_PASS_SLICES = ((0, 256), (256, 256), (512, 512))
 
-SEED_KIB = 52
-CUT = 768
-FIRST_PIECE = 32
+PIECES = {
+    "a0": (0, 2, 0, QUARTER, 2),
+    "a1": (0, 2, QUARTER, QUARTER, 3),
+    "c0": (2, 1, 0, HALF, 6),
+    "b1": (1, 1, HALF, HALF, 7),
+    "b0": (0, 1, HALF, HALF, 0),
+    "b2": (2, 1, HALF, HALF, 1),
+}
+
+SEED_KIB = 50
 PLACE = {
-    "w_raw00": 0, "w_raw01": 8, "flat": 16, "seed": 16, "tab_word1": 18, "floor0": 26, "w_raw10": 34, "w_raw11": 42,
-    "floor1": 50, "floor2": 58, "wm_scale": 66, "wm_word": 67,
-    "tab_word0": 136, "v_word0": 74, "w_bf00": 78,
-    "w_scale00": 82, "w_bf01": 83, "v_word1": 8,
-    "w_bf10": 83,
+    "w_raw00": 0, "w_raw01": 8, "flat": 16, "one": 16, "seed": 18, "tab_word1": 18, "floor0": 26,
+    "w_raw10": 34, "w_raw11": 42, "floor1": 153, "floor2": 161, "wm_scale": 66, "wm_word": 67,
+    "tab_word0": 160, "v_word0": 74, "w_bf00": 78, "w_bf01": 83, "v_word1": 8, "w_bf10": 83,
     "sq_bf00": 87, "sq_bf01": 92, "sq_bf10": 96, "sq_bf11": 100,
-    "zero00": 128, "w_bf11": 128,
-    "zero01": 104, "sq_scale00": 91.5, "zero_ws": 91.9375,
-    "picked00": 42,
-    "picked11": 105, "zero_first": 105.9375, "sq_scale01": 106,
-    "zero10": 107, "picked10": 107,
-    "picked20": 111, "zero11": 114.9375, "logs0": 115,
-    "logs1": 121,
-    "sq_scale10": 127, "sq_scale11": 127.5,
+    "zero00": 128, "w_bf11": 128, "sq_scale00": 91.5, "zero_ws": 91.9375,
+    "sq_scale01": 104, "sq_scale10": 104.5,
+    "picked01_first": 105, "picked01_rest": 107, "picked2_first": 113, "picked2_rest": 114,
+    "logs_a0": 117, "sq_scale11": 148, "logs_a1": 119, "logs_c0": 121, "logs_b0": 123, "logs_b1": 125,
+    "logs_b2": 132,
+    "result_a0": 136, "result_a1": 138, "result_c0_first": 140, "result_c0_rest": 113,
+    "result_b0": 142, "result_b1": 144, "result_b2": 146,
 }
 
 
@@ -66,19 +68,12 @@ def tile_list_voiced_log_spectra_kernel(tc, tab_words, tab_scales, offs, wc, ws,
         psum = ctx.enter_context(tc.psum_pool(name="psum", bufs=1))
 
         offsets = keep.tile([P, S // LIST_ROWS], U16, name="offsets")
+        flat_picked = keep.tile([P, S], U8, name="flat_picked", align_bytes=64)
         v_scale = [keep.tile([P, S], U8, name=f"v_scale{a}", align_bytes=64) for a in range(PASSES)]
         w_word = [[keep.tile([P, H], U32, name=f"w_word{f}{a}", align_bytes=64) for a in range(PASSES)] for f in (COS, SIN)]
-        w_scale_kept = {
-            (f, a): keep.tile([P, H], U8, name=f"w_scale{f}{a}", align_bytes=64)
-            for a in range(PASSES)
-            for f in (COS, SIN)
-            if (f, a) != (COS, 0)
-        }
-        sq_word = [keep.tile([P, S], U32, name=f"sq_word{f}", align_bytes=64) for f in (COS, SIN)]
+        w_scale = [[keep.tile([P, H], U8, name=f"w_scale{f}{a}", align_bytes=64) for a in range(PASSES)] for f in (COS, SIN)]
+        sq_word = [[keep.tile([P, HALF], U32, name=f"sq_word{f}{h}", align_bytes=64) for h in range(2)] for f in (COS, SIN)]
         warm = keep.tile([P, ONES], F32, name="warm", align_bytes=64)
-        result = keep.tile([P, BAND_TILES, S], F32, name="result", align_bytes=64)
-        warm_in = keep.tile([P, ONES], F32, name="warm_in", align_bytes=64)
-        one = keep.tile([P, ONES], F32, name="one", align_bytes=64)
 
         made = {}
 
@@ -102,39 +97,41 @@ def tile_list_voiced_log_spectra_kernel(tc, tab_words, tab_scales, offs, wc, ws,
         def sq_bf(f, h):
             return placed(f"sq_bf{f}{h}", [P, HALF, PACK], BF16)
 
-        def picked(i):
-            return placed(f"picked{i}0", [P, S], F32)
-
-        def picked_part(i, lo, n):
-            if i == 1 and lo < CUT:
-                return placed("picked10", [P, CUT], F32)[:, lo : lo + n]
-            if i == 1:
-                return placed("picked11", [P, S - CUT], F32)[:, lo - CUT : lo - CUT + n]
-            return picked(i)[:, lo : lo + n]
-
         def sq_scale(f, h):
             return placed(f"sq_scale{f}{h}", [P, HALF], U8)
-
-        def zero(f, h):
-            return placed(f"zero{f}{h}", [P, 32], F32)
-
-        def zero_ws():
-            return placed("zero_ws", [P, 32], F32)
-
-        def zero_first():
-            return placed("zero_first", [P, 32], F32)
-
-        def logs(h):
-            return placed(f"logs{h}", [P, BAND_TILES, HALF], F32)
 
         def v_word(a):
             return placed(f"v_word{a}", [P, S], U32)
 
-        def w_scale(f, a):
-            return placed("w_scale00", [P, H], U8) if (f, a) == (COS, 0) else w_scale_kept[(f, a)]
+        def picked_pair(lo, n):
+            if lo < QUARTER:
+                return placed("picked01_first", [P, 2, QUARTER], F32)[:, :, lo : lo + n]
+            return placed("picked01_rest", [P, 2, S - QUARTER], F32)[:, :, lo - QUARTER : lo - QUARTER + n]
+
+        def picked(i, lo, n):
+            if i < 2:
+                return picked_pair(lo, n)[:, i, :]
+            if lo < QUARTER:
+                return placed("picked2_first", [P, QUARTER], F32)[:, lo : lo + n]
+            return placed("picked2_rest", [P, S - QUARTER], F32)[:, lo - QUARTER : lo - QUARTER + n]
+
+        def logs(piece):
+            return placed(f"logs_{piece}", [P, HALF], F32)
+
+        def held(name):
+            if name in ("zero00", "zero_ws"):
+                return placed(name, [P, 32], F32)[:, 0:ONES]
+            return {
+                "sin1": picked(1, 0, ONES),
+                "sin2": sq_scale(COS, 1)[:, 0:32].bitcast(F32),
+                "sin3": picked(1, QUARTER, ONES),
+                "sin6": picked(2, 0, ONES),
+                "sin7": picked(2, QUARTER, ONES),
+                "early_log": sq_bf(SIN, 1)[:].rearrange("p j t -> p (j t)").bitcast(F32)[:, 512 : 512 + ONES],
+            }[name]
 
         tab_scale = placed("flat", [P, T // 4], I32)
-        flat_picked = keep.tile([P, S], U8, name="flat_picked", align_bytes=64)
+        seed = placed("seed", [P, SEED_KIB * 256], F32)
 
         def load_tab_words(a):
             nc.sync.dma_start(out=tab_word(a)[:], in_=tab_words[a].rearrange("p t i -> p (t i)").bitcast(I32))
@@ -146,9 +143,6 @@ def tile_list_voiced_log_spectra_kernel(tc, tab_words, tab_scales, offs, wc, ws,
         def load_floor(i):
             nc.sync.dma_start(out=floor(i)[:], in_=gT[P * i : P * (i + 1), :])
 
-        def load_tab_scales():
-            nc.sync.dma_start(out=tab_scale[0:32, :], in_=tab_scales.rearrange("a q t -> (a q) t").bitcast(I32))
-
         def move_scales(a, q):
             src = flat_picked[16 * a + 4 * q : 16 * a + 4 * q + 4, :].bitcast(I32)
             dst = v_scale[a][32 * q + 4 * a : 32 * q + 4 * a + 4, :].bitcast(I32)
@@ -157,38 +151,29 @@ def tile_list_voiced_log_spectra_kernel(tc, tab_words, tab_scales, offs, wc, ws,
             else:
                 nc.sync.dma_start(out=dst, in_=src)
 
-        def load_wm():
-            nc.sync.dma_start(out=wm_word[:].bitcast(I32), in_=wm_words[0].bitcast(I32))
-            for q in range(QUADRANTS):
-                nc.sync.dma_start(out=wm_scale[32 * q : 32 * q + 4, :], in_=wm_scales[0, 4 * q : 4 * q + 4, :].bitcast(I32))
-
         def list_slice(lo, n):
             return offsets[:, lo // LIST_ROWS : (lo + n) // LIST_ROWS]
 
         def gather_words(a, lo, n):
             nc.vector.tensor_copy(out=v_word(a)[:, lo : lo + n], in_=tab_word(a)[:].bitcast(U32).indirect(list_slice(lo, n)))
 
-        def gather_scales():
-            nc.vector.tensor_copy(out=flat_picked[:], in_=tab_scale[:].bitcast(U8).indirect(list_slice(0, S)))
-
         def gather_floor(i, lo, n):
-            nc.vector.tensor_copy(out=picked_part(i, lo, n), in_=floor(i)[:].indirect(list_slice(lo, n)))
+            nc.vector.tensor_copy(out=picked(i, lo, n), in_=floor(i)[:].indirect(list_slice(lo, n)))
 
         def round_w(f, a):
             src = w_raw(f, a)[:].rearrange("p j (m t) -> p m j t", t=PACK)
             dst = w_bf(f, a)[:].rearrange("p t m j -> p m j t")
             cut = SCALAR_SHARE[(f, a)]
             if (f, a) == (SIN, 1):
-                nc.scalar.activation(out=dst[:, 0:cut], in_=src[:, 0:cut], func=ACT.Identity, bias=zero_ws()[:, 0:1])
+                nc.scalar.activation(out=dst[:, 0:cut], in_=src[:, 0:cut], func=ACT.Identity, bias=held("zero_ws")[:, 0:1])
             elif cut > 0:
                 nc.scalar.activation(out=dst[:, 0:cut], in_=src[:, 0:cut], func=ACT.Copy)
-            if cut < P:
-                nc.vector.tensor_copy(out=dst[:, cut:P], in_=src[:, cut:P])
+            nc.vector.tensor_copy(out=dst[:, cut:P], in_=src[:, cut:P])
 
         def quantise_w(f, a):
             nc.vector.quantize_mx(
                 out=w_word[f][a][:].bitcast(FP8X4),
-                scales=w_scale(f, a)[:],
+                scales=w_scale[f][a][:],
                 in_=w_bf(f, a)[:].rearrange("p t m j -> p (t m j)"),
             )
 
@@ -203,7 +188,7 @@ def tile_list_voiced_log_spectra_kernel(tc, tab_words, tab_scales, offs, wc, ws,
                 nc.tensor.matmul_mx(
                     out=sums[(f, b)][:, t, :],
                     lhsT=w_word[f][a][:, w_cols].bitcast(FP8X4),
-                    lhsT_scale=w_scale(f, a)[:, w_cols],
+                    lhsT_scale=w_scale[f][a][:, w_cols],
                     rhs=v_word(a)[:, frames].bitcast(FP8X4),
                     rhs_scale=v_scale[a][4 * a : P, frames],
                     start=(a == 0 and t == 0),
@@ -212,78 +197,97 @@ def tile_list_voiced_log_spectra_kernel(tc, tab_words, tab_scales, offs, wc, ws,
 
         def square(f, b):
             h, place_in_half = divmod(b, BLOCKS_PER_HALF)
+            bias = 0.0
+            if (f, h) == (COS, 0):
+                bias = held("zero00")[:, 0:1]
+            if f == SIN and b in (1, 2, 3, 6, 7):
+                bias = held(f"sin{b}")[:, 0:1]
             nc.scalar.activation(
                 out=sq_bf(f, h)[:, BLOCK * place_in_half : BLOCK * (place_in_half + 1), :],
                 in_=sums[(f, b)][:].rearrange("p t j -> p j t"),
                 func=ACT.Square,
-                bias=(zero_first() if (f, b) == (SIN, 0) else zero(f, h))[:, 0:1],
+                bias=bias,
             )
 
         def open_first_products(f):
             for b in range(AHEAD[f]):
                 first_pass(f, b, 0)
 
-        def first_products(f, h):
-            for b in range(BLOCKS_PER_HALF * h, BLOCKS_PER_HALF * (h + 1)):
+        def first_products(f, blocks):
+            for b in blocks:
                 first_pass(f, b, 1)
                 square(f, b)
                 if b + AHEAD[f] < S // BLOCK:
                     first_pass(f, b + AHEAD[f], 0)
 
-        def quantise_squares(f, h):
-            frames = slice(HALF * h, HALF * (h + 1))
+        def quantise_squares(f, lo, n):
+            h, first = divmod(lo, HALF)
+            cols = slice(first, first + n)
             nc.vector.quantize_mx(
-                out=sq_word[f][:, frames].bitcast(FP8X4),
-                scales=sq_scale(f, h)[:],
-                in_=sq_bf(f, h)[:].rearrange("p j t -> p (j t)"),
+                out=sq_word[f][h][:, cols].bitcast(FP8X4),
+                scales=sq_scale(f, h)[:, cols],
+                in_=sq_bf(f, h)[:, cols, :].rearrange("p j t -> p (j t)"),
             )
 
         power = {}
 
-        def second_pass(h, i, f):
-            frames = slice(HALF * h, HALF * (h + 1))
-            if f == SIN - h:
-                power[(h, i)] = psum.tile([P, HALF], F32, name="power", tag=f"bank{POWER_BANK[h][i]}")
-            nc.tensor.matmul_mx(
-                out=power[(h, i)][:],
-                lhsT=wm_word[:, 2 * P * i : 2 * P * (i + 1)].bitcast(FP4X4),
-                lhsT_scale=wm_scale[:].bitcast(U8)[:, P * i : P * (i + 1)],
-                rhs=sq_word[f][:, frames].bitcast(FP8X4),
-                rhs_scale=sq_scale(f, h)[:],
-                start=(f == SIN - h),
-                stop=(f == h),
+        def second_passes(piece, f):
+            first_band, bands, lo, n, bank = PIECES[piece]
+            h, first = divmod(lo, HALF)
+            cols = slice(first, first + n)
+            if f == COS:
+                power[piece] = psum.tile([P, HALF], F32, name="power", tag=f"bank{bank}")
+            for k in range(bands):
+                i = first_band + k
+                nc.tensor.matmul_mx(
+                    out=power[piece][:, n * k : n * (k + 1)],
+                    lhsT=wm_word[:, 2 * P * i : 2 * P * (i + 1)].bitcast(FP4X4),
+                    lhsT_scale=wm_scale[:].bitcast(U8)[:, P * i : P * (i + 1)],
+                    rhs=sq_word[f][h][:, cols].bitcast(FP8X4),
+                    rhs_scale=sq_scale(f, h)[:, cols],
+                    start=(f == COS and k == 0),
+                    stop=(f == SIN and k == bands - 1),
+                )
+
+        def logarithm(piece):
+            scale = held("early_log")[:, 0:1] if piece == "a0" else 1.0
+            nc.scalar.activation(out=logs(piece)[:], in_=power[piece][:], func=ACT.Ln, bias=one[:, 0:1], scale=scale)
+
+        def subtract_two_bands(engine, piece):
+            lo = PIECES[piece][2]
+            result = placed(f"result_{piece}", [P, 2, QUARTER], F32)
+            engine.tensor_tensor(
+                out=result[:],
+                in0=logs(piece)[:].rearrange("p (i j) -> p i j", i=2),
+                in1=picked_pair(lo, QUARTER),
+                op=ALU.subtract,
             )
+            nc.sync.dma_start(out=out[0 : 2 * P, lo : lo + QUARTER].rearrange("(i p) j -> p i j", p=P), in_=result[:])
 
-        def logarithm(h, i):
-            nc.scalar.activation(out=logs(h)[:, i, :], in_=power[(h, i)][:], func=ACT.Ln, bias=one[:, 0:1])
-
-        def subtract_and_store(engine, h, i, lo, n):
-            part = slice(lo, lo + n)
-            frames = slice(HALF * h + lo, HALF * h + lo + n)
-            engine.tensor_tensor(out=result[:, i, frames], in0=logs(h)[:, i, part], in1=picked_part(i, HALF * h + lo, n), op=ALU.subtract)
-            nc.sync.dma_start(out=out[P * i : P * (i + 1), frames], in_=result[:, i, frames])
+        def subtract_band(engine, piece, result, first, n, place):
+            i, lo = PIECES[piece][0], PIECES[piece][2] + first
+            dst = result[:, place : place + n]
+            engine.tensor_tensor(out=dst, in0=logs(piece)[:, first : first + n], in1=picked(i, lo, n), op=ALU.subtract)
+            nc.sync.dma_start(out=out[P * i : P * (i + 1), lo : lo + n], in_=dst)
 
         nc.sync.dma_start(offsets[:], offs)
         nc.vector.memset(tab_scale[32:64, :], 0)
         nc.vector.memset(tab_scale[64:P, :], 0)
-        nc.vector.memset(warm_in[:], 1.0)
+        nc.vector.memset(seed[:, 0:ONES], 1.0)
         for a in range(PASSES):
             nc.vector.memset(v_scale[a][:].bitcast(I32), 0)
-        for f in (COS, SIN):
-            for h in range(S // HALF):
-                nc.gpsimd.memset(zero(f, h)[:, 0:ONES], 0.0)
-        nc.gpsimd.memset(zero_first()[:], 0.0)
-        nc.gpsimd.memset(zero_ws()[:], 0.0)
-        nc.scalar.activation(out=warm[:], in_=warm_in[:], func=ACT.Ln)
+        for name in ("zero00", "zero_ws", "sin1", "sin2", "sin3", "sin6", "sin7"):
+            nc.gpsimd.memset(held(name), 0.0)
+        nc.gpsimd.memset(held("early_log"), 1.0)
+        nc.scalar.activation(out=warm[:], in_=seed[:, 0:ONES], func=ACT.Ln)
 
-        load_tab_scales()
+        nc.sync.dma_start(out=tab_scale[0:32, :], in_=tab_scales.rearrange("a q t -> (a q) t").bitcast(I32))
         load_tab_words(0)
         load_w(COS, 0)
         load_w(COS, 1)
-        gather_scales()
-        seed = placed("seed", [P, SEED_KIB * 256], F32)
-        nc.gpsimd.memset(seed[:, 0:ONES], 1.0)
-        nc.gpsimd.tensor_copy(out=one[:], in_=seed[:, 0:ONES])
+        nc.vector.tensor_copy(out=flat_picked[:], in_=tab_scale[:].bitcast(U8).indirect(list_slice(0, S)))
+        one = placed("one", [P, ONES], F32)
+        nc.vector.tensor_copy(out=one[:], in_=seed[:, 0:ONES])
         wm_word = placed("wm_word", [P, 2 * N], U8)
         wm_scale = placed("wm_scale", [P, N // 4], I32)
         nc.gpsimd.memset(wm_scale[:], 0)
@@ -295,8 +299,10 @@ def tile_list_voiced_log_spectra_kernel(tc, tab_words, tab_scales, offs, wc, ws,
         load_w(SIN, 0)
         load_w(SIN, 1)
         load_floor(0)
+        nc.sync.dma_start(out=wm_word[:].bitcast(I32), in_=wm_words[0].bitcast(I32))
+        for q in range(QUADRANTS):
+            nc.sync.dma_start(out=wm_scale[32 * q : 32 * q + 4, :], in_=wm_scales[0, 4 * q : 4 * q + 4, :].bitcast(I32))
         load_floor(1)
-        load_wm()
         load_floor(2)
 
         gather_words(0, 0, S)
@@ -310,36 +316,46 @@ def tile_list_voiced_log_spectra_kernel(tc, tab_words, tab_scales, offs, wc, ws,
             gather_words(1, lo, n)
         round_w(SIN, 0)
         quantise_w(SIN, 0)
-        first_products(COS, 0)
+        first_products(COS, range(4))
         round_w(SIN, 1)
-        quantise_squares(COS, 0)
+        quantise_squares(COS, 0, HALF)
         quantise_w(SIN, 1)
-        gather_floor(0, 0, S)
-        first_products(COS, 1)
+        gather_floor(0, 0, QUARTER)
+        gather_floor(0, QUARTER, S - QUARTER)
+        first_products(COS, range(4, 8))
         open_first_products(SIN)
-        first_products(SIN, 0)
-        quantise_squares(COS, 1)
-        gather_floor(1, CUT, S - CUT)
-        quantise_squares(SIN, 0)
-        gather_floor(1, 0, CUT)
-        first_products(SIN, 1)
-        quantise_squares(SIN, 1)
-        for h in range(S // HALF):
-            gather_floor(2, HALF * h, HALF)
+        first_products(SIN, range(5))
+        quantise_squares(SIN, 0, QUARTER)
+        gather_floor(1, 0, QUARTER)
+        quantise_squares(COS, HALF, HALF)
+        quantise_squares(SIN, QUARTER, QUARTER)
+        gather_floor(1, QUARTER, S - QUARTER)
+        first_pass(SIN, 5, 1)
+        for f in (COS, SIN):
+            second_passes("a0", f)
+        for b in range(6, 8):
+            first_pass(SIN, b, 1)
+        logarithm("a0")
+        subtract_two_bands(nc.gpsimd, "a0")
+        for b in range(5, 8):
+            square(SIN, b)
+        gather_floor(2, 0, QUARTER)
+        quantise_squares(SIN, HALF, HALF)
+        gather_floor(2, QUARTER, S - QUARTER)
 
-        for i in range(BAND_TILES):
-            second_pass(0, i, SIN)
-            second_pass(0, i, COS)
-            logarithm(0, i)
-        for i in (1, 0, 2):
-            second_pass(1, i, COS)
-        for i in (1, 0, 2):
-            second_pass(1, i, SIN)
-            logarithm(1, i)
-        subtract_and_store(nc.gpsimd, 0, 0, 0, HALF)
-        subtract_and_store(nc.gpsimd, 0, 1, 0, HALF)
-        subtract_and_store(nc.vector, 0, 2, 0, HALF)
-        subtract_and_store(nc.vector, 1, 1, 0, 256)
-        subtract_and_store(nc.vector, 1, 0, 0, HALF)
-        subtract_and_store(nc.vector, 1, 2, 0, HALF)
-        subtract_and_store(nc.vector, 1, 1, 256, 256)
+        for piece in ("a1", "c0"):
+            for f in (COS, SIN):
+                second_passes(piece, f)
+            logarithm(piece)
+        for f in (COS, SIN):
+            for piece in ("b1", "b0", "b2"):
+                second_passes(piece, f)
+        for piece in ("b1", "b0", "b2"):
+            logarithm(piece)
+        subtract_two_bands(nc.gpsimd, "a1")
+        subtract_band(nc.gpsimd, "c0", placed("result_c0_first", [P, QUARTER], F32), 0, QUARTER, 0)
+        subtract_band(nc.vector, "b1", placed("result_b1", [P, HALF], F32), 0, HALF, 0)
+        subtract_band(nc.vector, "c0", placed("result_c0_rest", [P, QUARTER], F32), QUARTER, QUARTER, 0)
+        subtract_band(nc.vector, "b0", placed("result_b0", [P, HALF], F32), 0, HALF, 0)
+        for first in (0, QUARTER):
+            subtract_band(nc.vector, "b2", placed("result_b2", [P, HALF], F32), first, QUARTER, first)

@@ -30,7 +30,7 @@ LIST_ROWS = 16
 ONES = 8
 
 QUARTER = 256
-SUM_BANK = ((0, 1, 2, 3, 0, 1, 2, 3), (4, 5, 6, 7, 0, 1, 4, 5))
+SUM_BANK = ((0, 1, 2, 3, 0, 1, 2, 3), (4, 5, 6, 7, 0, 1, 7, 0))
 AHEAD = (4, 6)
 SCALAR_SHARE = {(COS, 0): 88, (COS, 1): 72, (SIN, 0): 0, (SIN, 1): 40}
 SECOND_PASS_SLICES = ((0, 256), (256, 256), (512, 512))
@@ -38,9 +38,9 @@ SECOND_PASS_SLICES = ((0, 256), (256, 256), (512, 512))
 PIECES = {
     "a0": (0, 2, 0, QUARTER, 2),
     "a1": (0, 2, QUARTER, QUARTER, 3),
-    "c0": (2, 1, 0, HALF, 6),
-    "b1": (1, 1, HALF, HALF, 7),
-    "b0": (0, 1, HALF, HALF, 0),
+    "c0": (2, 1, 0, HALF, 4),
+    "b1": (1, 1, HALF, HALF, 5),
+    "b0": (0, 1, HALF, HALF, 6),
     "b2": (2, 1, HALF, HALF, 1),
 }
 
@@ -52,7 +52,7 @@ PLACE = {
     "sq_bf00": 87, "sq_bf01": 92, "sq_bf10": 96, "sq_bf11": 100,
     "zero00": 128, "w_bf11": 128, "sq_scale00": 91.5, "zero_ws": 91.9375,
     "sq_scale01": 104, "sq_scale10": 104.5,
-    "picked01_first": 105, "picked01_rest": 107, "picked2_first": 113, "picked2_rest": 114,
+    "picked01": 105, "picked2_first": 113, "picked2_rest": 114,
     "logs_a0": 117, "sq_scale11": 148, "logs_a1": 119, "logs_c0": 121, "logs_b0": 123, "logs_b1": 125,
     "logs_b2": 132,
     "result_a0": 136, "result_a1": 138, "result_c0_first": 140, "result_c0_rest": 113,
@@ -104,9 +104,7 @@ def tile_list_voiced_log_spectra_kernel(tc, tab_words, tab_scales, offs, wc, ws,
             return placed(f"v_word{a}", [P, S], U32)
 
         def picked_pair(lo, n):
-            if lo < QUARTER:
-                return placed("picked01_first", [P, 2, QUARTER], F32)[:, :, lo : lo + n]
-            return placed("picked01_rest", [P, 2, S - QUARTER], F32)[:, :, lo - QUARTER : lo - QUARTER + n]
+            return placed("picked01", [P, 2, S], F32)[:, :, lo : lo + n]
 
         def picked(i, lo, n):
             if i < 2:
@@ -127,7 +125,7 @@ def tile_list_voiced_log_spectra_kernel(tc, tab_words, tab_scales, offs, wc, ws,
                 "sin3": picked(1, QUARTER, ONES),
                 "sin6": picked(2, 0, ONES),
                 "sin7": picked(2, QUARTER, ONES),
-                "early_log": sq_bf(SIN, 1)[:].rearrange("p j t -> p (j t)").bitcast(F32)[:, 512 : 512 + ONES],
+                "early_log": sq_bf(SIN, 1)[:].rearrange("p j t -> p (j t)").bitcast(F32)[:, 256 : 256 + ONES],
             }[name]
 
         tab_scale = placed("flat", [P, T // 4], I32)
@@ -217,7 +215,7 @@ def tile_list_voiced_log_spectra_kernel(tc, tab_words, tab_scales, offs, wc, ws,
             for b in blocks:
                 first_pass(f, b, 1)
                 square(f, b)
-                if b + AHEAD[f] < S // BLOCK:
+                if f == COS and b + AHEAD[f] < S // BLOCK:
                     first_pass(f, b + AHEAD[f], 0)
 
         def quantise_squares(f, lo, n):
@@ -320,8 +318,7 @@ def tile_list_voiced_log_spectra_kernel(tc, tab_words, tab_scales, offs, wc, ws,
         round_w(SIN, 1)
         quantise_squares(COS, 0, HALF)
         quantise_w(SIN, 1)
-        gather_floor(0, 0, QUARTER)
-        gather_floor(0, QUARTER, S - QUARTER)
+        gather_floor(0, 0, S)
         first_products(COS, range(4, 8))
         open_first_products(SIN)
         first_products(SIN, range(5))
@@ -334,7 +331,8 @@ def tile_list_voiced_log_spectra_kernel(tc, tab_words, tab_scales, offs, wc, ws,
         for f in (COS, SIN):
             second_passes("a0", f)
         for b in range(6, 8):
-            first_pass(SIN, b, 1)
+            for a in range(PASSES):
+                first_pass(SIN, b, a)
         logarithm("a0")
         subtract_two_bands(nc.gpsimd, "a0")
         for b in range(5, 8):

@@ -120,8 +120,8 @@ def tile_list_voiced_log_spectra_kernel(tc, tab_words, tab_scales, offs, wc, ws,
             if name in ("zero00", "zero_ws"):
                 return placed(name, [P, 32], F32)[:, 0:ONES]
             return {
-                "sin1": picked(1, 0, ONES),
-                "sin2": sq_scale(COS, 1)[:, 0:32].bitcast(F32),
+                "sin1": sq_scale(COS, 1)[:, 0:32].bitcast(F32),
+                "sin2": picked(1, 0, ONES),
                 "sin3": picked(1, QUARTER, ONES),
                 "sin6": picked(2, 0, ONES),
                 "sin7": picked(2, QUARTER, ONES),
@@ -323,8 +323,8 @@ def tile_list_voiced_log_spectra_kernel(tc, tab_words, tab_scales, offs, wc, ws,
         open_first_products(SIN)
         first_products(SIN, range(5))
         quantise_squares(SIN, 0, QUARTER)
-        gather_floor(1, 0, QUARTER)
         quantise_squares(COS, HALF, HALF)
+        gather_floor(1, 0, QUARTER)
         quantise_squares(SIN, QUARTER, QUARTER)
         gather_floor(1, QUARTER, S - QUARTER)
         first_pass(SIN, 5, 1)

@@ -30,33 +30,43 @@ LIST_ROWS = 16
 ONES = 8
 
 QUARTER = 256
-SUM_BANK = ((0, 1, 2, 3, 0, 1, 2, 3), (4, 5, 6, 7, 0, 1, 7, 0))
+BLOCKS = S // BLOCK
+BANKS = 8
 AHEAD = (4, 6)
-SCALAR_SHARE = {(COS, 0): 88, (COS, 1): 72, (SIN, 0): 0, (SIN, 1): 40}
-SECOND_PASS_SLICES = ((0, 256), (256, 256), (512, 512))
+SCALAR_SHARE = {(COS, 0): 72, (COS, 1): 56, (SIN, 0): 0, (SIN, 1): 40}
+SECOND_PASS_SLICES = ((0, BLOCK), (BLOCK, BLOCK), (QUARTER, QUARTER), (HALF, HALF))
 
 PIECES = {
-    "a0": (0, 2, 0, QUARTER, 2),
-    "a1": (0, 2, QUARTER, QUARTER, 3),
-    "c0": (2, 1, 0, HALF, 4),
-    "b1": (1, 1, HALF, HALF, 5),
-    "b0": (0, 1, HALF, HALF, 6),
-    "b2": (2, 1, HALF, HALF, 1),
+    "pair0": (0, 2, 0, QUARTER, (COS, 6)),
+    "pair1": (0, 2, QUARTER, QUARTER, (COS, 7)),
+    "early2": (2, 1, 0, HALF, (SIN, 0)),
+    "late1": (1, 1, HALF, HALF, (SIN, 1)),
+    "late0": (0, 1, HALF, HALF, (SIN, 2)),
+    "late2": (2, 1, HALF, HALF, (SIN, 5)),
 }
 
-SEED_KIB = 50
+BIG = 8192
+GAP = 2048
+SMALL = 128
+FLOORS = 3 * BIG + GAP
+BEHIND = FLOORS + BAND_TILES * BIG
 PLACE = {
-    "w_raw00": 0, "w_raw01": 8, "flat": 16, "one": 16, "seed": 18, "tab_word1": 18, "floor0": 26,
-    "w_raw10": 34, "w_raw11": 42, "floor1": 153, "floor2": 161, "wm_scale": 66, "wm_word": 67,
-    "tab_word0": 160, "v_word0": 74, "w_bf00": 78, "w_bf01": 83, "v_word1": 8, "w_bf10": 83,
-    "sq_bf00": 87, "sq_bf01": 92, "sq_bf10": 96, "sq_bf11": 100,
-    "zero00": 128, "w_bf11": 128, "sq_scale00": 91.5, "zero_ws": 91.9375,
-    "sq_scale01": 104, "sq_scale10": 104.5,
-    "picked01": 105, "picked2_first": 113, "picked2_rest": 114,
-    "logs_a0": 117, "sq_scale11": 148, "logs_a1": 119, "logs_c0": 121, "logs_b0": 123, "logs_b1": 125,
-    "logs_b2": 132,
-    "result_a0": 136, "result_a1": 138, "result_c0_first": 140, "result_c0_rest": 113,
-    "result_b0": 142, "result_b1": 144, "result_b2": 146,
+    "tab_word1": 0,
+    "w_raw10": BIG,
+    "w_raw11": 2 * BIG,
+    "wm_scale": 3 * BIG,
+    "wm_word": 3 * BIG + GAP // 2,
+    "floor0": FLOORS,
+    "floor1": FLOORS + BIG,
+    "floor2": FLOORS + 2 * BIG,
+    "tab_scale": BIG - GAP // 2,
+    "tab_word0": 3 * BIG - BIG // 2,
+    "w_raw00": FLOORS + 2 * BIG - BIG // 2,
+    "w_raw01": BEHIND,
+    "v_word1": BEHIND,
+    "sq_scale00": BEHIND + BIG,
+    "share_zero": BEHIND + BIG + HALF - SMALL // 2,
+    "sq_bf_cos768": BEHIND + BIG + HALF,
 }
 
 
@@ -64,72 +74,72 @@ def tile_list_voiced_log_spectra_kernel(tc, tab_words, tab_scales, offs, wc, ws,
     nc = tc.nc
     with ExitStack() as ctx:
         keep = ctx.enter_context(tc.tile_pool(name="keep", bufs=1))
-        work = ctx.enter_context(tc.tile_pool(name="work", bufs=1))
+        area = ctx.enter_context(tc.tile_pool(name="area", bufs=1))
         psum = ctx.enter_context(tc.psum_pool(name="psum", bufs=1))
 
         offsets = keep.tile([P, S // LIST_ROWS], U16, name="offsets")
-        flat_picked = keep.tile([P, S], U8, name="flat_picked", align_bytes=64)
-        v_scale = [keep.tile([P, S], U8, name=f"v_scale{a}", align_bytes=64) for a in range(PASSES)]
-        w_word = [[keep.tile([P, H], U32, name=f"w_word{f}{a}", align_bytes=64) for a in range(PASSES)] for f in (COS, SIN)]
-        w_scale = [[keep.tile([P, H], U8, name=f"w_scale{f}{a}", align_bytes=64) for a in range(PASSES)] for f in (COS, SIN)]
-        sq_word = [[keep.tile([P, HALF], U32, name=f"sq_word{f}{h}", align_bytes=64) for h in range(2)] for f in (COS, SIN)]
-        warm = keep.tile([P, ONES], F32, name="warm", align_bytes=64)
-
         made = {}
 
-        def placed(name, shape, dtype):
+        def sb(name, shape, dtype, tag=None):
+            if name not in made and name in PLACE:
+                made[name] = area.tile(shape, dtype, name=name, offset=PLACE[name], align_bytes=64)
             if name not in made:
-                made[name] = work.tile(shape, dtype, name=name, offset=int(1024 * PLACE[name]), align_bytes=64)
+                made[name] = keep.tile(shape, dtype, name=name, tag=tag or name, align_bytes=64)
             return made[name]
 
         def tab_word(a):
-            return placed(f"tab_word{a}", [P, T], I32)
+            return sb(f"tab_word{a}", [P, T], I32)
 
         def w_raw(f, a):
-            return placed(f"w_raw{f}{a}", [P, PACK, H], F32)
+            return sb(f"w_raw{f}{a}", [P, PACK, H], F32)
 
         def floor(i):
-            return placed(f"floor{i}", [P, T], F32)
+            return sb(f"floor{i}", [P, T], F32)
 
         def w_bf(f, a):
-            return placed(f"w_bf{f}{a}", [P, PACK, P, PACK], BF16)
+            tag = "w_bf01" if (f, a) == (SIN, 0) else None
+            return sb(f"w_bf{f}{a}", [P, PACK, P, PACK], BF16, tag)
 
-        def sq_bf(f, h):
-            return placed(f"sq_bf{f}{h}", [P, HALF, PACK], BF16)
+        def w_word(f, a):
+            return sb(f"w_word{f}{a}", [P, H], U32)
 
-        def sq_scale(f, h):
-            return placed(f"sq_scale{f}{h}", [P, HALF], U8)
+        def w_scale(f, a):
+            return sb(f"w_scale{f}{a}", [P, H], U8)
 
         def v_word(a):
-            return placed(f"v_word{a}", [P, S], U32)
+            return sb(f"v_word{a}", [P, S], U32)
+
+        def v_scale(a):
+            return sb(f"v_scale{a}", [P, S], U8)
+
+        def sq_bf(f, lo, n):
+            if f == COS and lo >= HALF:
+                first = lo - lo % QUARTER
+                return sb(f"sq_bf_cos{first}", [P, QUARTER, PACK], BF16)[:, lo - first : lo - first + n, :]
+            first = lo - lo % HALF
+            return sb(f"sq_bf{f}{first // HALF}", [P, HALF, PACK], BF16)[:, lo - first : lo - first + n, :]
+
+        def block_column(f, b):
+            return sq_bf(f, BLOCK * b, BLOCK).rearrange("p j t -> p (j t)").bitcast(F32)[:, 0:ONES]
+
+        def sq_word(f, h):
+            return sb(f"sq_word{f}{h}", [P, HALF], U32)
+
+        def sq_scale(f, h):
+            return sb(f"sq_scale{f}{h}", [P, HALF], U8)
 
         def picked_pair(lo, n):
-            return placed("picked01", [P, 2, S], F32)[:, :, lo : lo + n]
+            return sb("picked01", [P, 2, S], F32)[:, :, lo : lo + n]
 
         def picked(i, lo, n):
             if i < 2:
                 return picked_pair(lo, n)[:, i, :]
             if lo < QUARTER:
-                return placed("picked2_first", [P, QUARTER], F32)[:, lo : lo + n]
-            return placed("picked2_rest", [P, S - QUARTER], F32)[:, lo - QUARTER : lo - QUARTER + n]
+                return sb("picked2_first", [P, QUARTER], F32)[:, lo : lo + n]
+            return sb("picked2_rest", [P, S - QUARTER], F32)[:, lo - QUARTER : lo - QUARTER + n]
 
         def logs(piece):
-            return placed(f"logs_{piece}", [P, HALF], F32)
-
-        def held(name):
-            if name in ("zero00", "zero_ws"):
-                return placed(name, [P, 32], F32)[:, 0:ONES]
-            return {
-                "sin1": sq_scale(COS, 1)[:, 0:32].bitcast(F32),
-                "sin2": picked(1, 0, ONES),
-                "sin3": picked(1, QUARTER, ONES),
-                "sin6": picked(2, 0, ONES),
-                "sin7": picked(2, QUARTER, ONES),
-                "early_log": sq_bf(SIN, 1)[:].rearrange("p j t -> p (j t)").bitcast(F32)[:, 256 : 256 + ONES],
-            }[name]
-
-        tab_scale = placed("flat", [P, T // 4], I32)
-        seed = placed("seed", [P, SEED_KIB * 256], F32)
+            return sb(f"logs_{piece}", [P, HALF], F32)
 
         def load_tab_words(a):
             nc.sync.dma_start(out=tab_word(a)[:], in_=tab_words[a].rearrange("p t i -> p (t i)").bitcast(I32))
@@ -143,7 +153,7 @@ def tile_list_voiced_log_spectra_kernel(tc, tab_words, tab_scales, offs, wc, ws,
 
         def move_scales(a, q):
             src = flat_picked[16 * a + 4 * q : 16 * a + 4 * q + 4, :].bitcast(I32)
-            dst = v_scale[a][32 * q + 4 * a : 32 * q + 4 * a + 4, :].bitcast(I32)
+            dst = v_scale(a)[32 * q + 4 * a : 32 * q + 4 * a + 4, :].bitcast(I32)
             if (a, q) == (0, 0):
                 nc.vector.tensor_copy(out=dst, in_=src)
             else:
@@ -163,48 +173,50 @@ def tile_list_voiced_log_spectra_kernel(tc, tab_words, tab_scales, offs, wc, ws,
             dst = w_bf(f, a)[:].rearrange("p t m j -> p m j t")
             cut = SCALAR_SHARE[(f, a)]
             if (f, a) == (SIN, 1):
-                nc.scalar.activation(out=dst[:, 0:cut], in_=src[:, 0:cut], func=ACT.Identity, bias=held("zero_ws")[:, 0:1])
+                nc.scalar.activation(out=dst[:, 0:cut], in_=src[:, 0:cut], func=ACT.Identity, bias=share_zero[:, 0:1], scale=share_one[:, 0:1])
             elif cut > 0:
                 nc.scalar.activation(out=dst[:, 0:cut], in_=src[:, 0:cut], func=ACT.Copy)
             nc.vector.tensor_copy(out=dst[:, cut:P], in_=src[:, cut:P])
 
         def quantise_w(f, a):
             nc.vector.quantize_mx(
-                out=w_word[f][a][:].bitcast(FP8X4),
-                scales=w_scale[f][a][:],
+                out=w_word(f, a)[:].bitcast(FP8X4),
+                scales=w_scale(f, a)[:],
                 in_=w_bf(f, a)[:].rearrange("p t m j -> p (t m j)"),
             )
+
+        def sum_bank(f, b):
+            if f == COS:
+                return b % AHEAD[COS]
+            if b < AHEAD[SIN]:
+                return (AHEAD[COS] + b) % BANKS
+            return sum_bank(SIN, b - 3)
 
         sums = {}
 
         def first_pass(f, b, a):
             frames = slice(BLOCK * b, BLOCK * (b + 1))
             if a == 0:
-                sums[(f, b)] = psum.tile([P, PACK, BLOCK], F32, name="sums", tag=f"bank{SUM_BANK[f][b]}")
+                sums[(f, b)] = psum.tile([P, PACK, BLOCK], F32, name="sums", tag=f"bank{sum_bank(f, b)}")
             for t in range(PACK):
                 w_cols = slice(P * t, P * (t + 1))
                 nc.tensor.matmul_mx(
                     out=sums[(f, b)][:, t, :],
-                    lhsT=w_word[f][a][:, w_cols].bitcast(FP8X4),
-                    lhsT_scale=w_scale[f][a][:, w_cols],
+                    lhsT=w_word(f, a)[:, w_cols].bitcast(FP8X4),
+                    lhsT_scale=w_scale(f, a)[:, w_cols],
                     rhs=v_word(a)[:, frames].bitcast(FP8X4),
-                    rhs_scale=v_scale[a][4 * a : P, frames],
+                    rhs_scale=v_scale(a)[4 * a : P, frames],
                     start=(a == 0 and t == 0),
                     stop=(a == PASSES - 1 and t == PACK - 1),
                 )
 
         def square(f, b):
-            h, place_in_half = divmod(b, BLOCKS_PER_HALF)
-            bias = 0.0
-            if (f, h) == (COS, 0):
-                bias = held("zero00")[:, 0:1]
-            if f == SIN and b in (1, 2, 3, 6, 7):
-                bias = held(f"sin{b}")[:, 0:1]
+            zero = zero_bias.get((f, b))
             nc.scalar.activation(
-                out=sq_bf(f, h)[:, BLOCK * place_in_half : BLOCK * (place_in_half + 1), :],
+                out=sq_bf(f, BLOCK * b, BLOCK),
                 in_=sums[(f, b)][:].rearrange("p t j -> p j t"),
                 func=ACT.Square,
-                bias=bias,
+                bias=0.0 if zero is None else zero[:, 0:1],
             )
 
         def open_first_products(f):
@@ -215,46 +227,46 @@ def tile_list_voiced_log_spectra_kernel(tc, tab_words, tab_scales, offs, wc, ws,
             for b in blocks:
                 first_pass(f, b, 1)
                 square(f, b)
-                if f == COS and b + AHEAD[f] < S // BLOCK:
+                if f == COS and b + AHEAD[f] < BLOCKS:
                     first_pass(f, b + AHEAD[f], 0)
 
         def quantise_squares(f, lo, n):
             h, first = divmod(lo, HALF)
             cols = slice(first, first + n)
             nc.vector.quantize_mx(
-                out=sq_word[f][h][:, cols].bitcast(FP8X4),
+                out=sq_word(f, h)[:, cols].bitcast(FP8X4),
                 scales=sq_scale(f, h)[:, cols],
-                in_=sq_bf(f, h)[:, cols, :].rearrange("p j t -> p (j t)"),
+                in_=sq_bf(f, lo, n).rearrange("p j t -> p (j t)"),
             )
 
         power = {}
 
         def second_passes(piece, f):
-            first_band, bands, lo, n, bank = PIECES[piece]
+            first_band, bands, lo, n, follows = PIECES[piece]
             h, first = divmod(lo, HALF)
             cols = slice(first, first + n)
             if f == COS:
-                power[piece] = psum.tile([P, HALF], F32, name="power", tag=f"bank{bank}")
+                power[piece] = psum.tile([P, HALF], F32, name="power", tag=f"bank{sum_bank(*follows)}")
             for k in range(bands):
                 i = first_band + k
                 nc.tensor.matmul_mx(
                     out=power[piece][:, n * k : n * (k + 1)],
                     lhsT=wm_word[:, 2 * P * i : 2 * P * (i + 1)].bitcast(FP4X4),
                     lhsT_scale=wm_scale[:].bitcast(U8)[:, P * i : P * (i + 1)],
-                    rhs=sq_word[f][h][:, cols].bitcast(FP8X4),
+                    rhs=sq_word(f, h)[:, cols].bitcast(FP8X4),
                     rhs_scale=sq_scale(f, h)[:, cols],
                     start=(f == COS and k == 0),
                     stop=(f == SIN and k == bands - 1),
                 )
 
         def logarithm(piece):
-            scale = held("early_log")[:, 0:1] if piece == "a0" else 1.0
-            nc.scalar.activation(out=logs(piece)[:], in_=power[piece][:], func=ACT.Ln, bias=one[:, 0:1], scale=scale)
+            ones = early_one if piece == "pair0" else one
+            nc.scalar.activation(out=logs(piece)[:], in_=power[piece][:], func=ACT.Ln, bias=ones[:, 0:1])
 
-        def subtract_two_bands(engine, piece):
+        def subtract_pair(piece):
             lo = PIECES[piece][2]
-            result = placed(f"result_{piece}", [P, 2, QUARTER], F32)
-            engine.tensor_tensor(
+            result = sb(f"result_{piece}", [P, 2, QUARTER], F32)
+            nc.gpsimd.tensor_tensor(
                 out=result[:],
                 in0=logs(piece)[:].rearrange("p (i j) -> p i j", i=2),
                 in1=picked_pair(lo, QUARTER),
@@ -262,50 +274,61 @@ def tile_list_voiced_log_spectra_kernel(tc, tab_words, tab_scales, offs, wc, ws,
             )
             nc.sync.dma_start(out=out[0 : 2 * P, lo : lo + QUARTER].rearrange("(i p) j -> p i j", p=P), in_=result[:])
 
-        def subtract_band(engine, piece, result, first, n, place):
+        def subtract_band(engine, piece, first, n, tag=None):
             i, lo = PIECES[piece][0], PIECES[piece][2] + first
-            dst = result[:, place : place + n]
-            engine.tensor_tensor(out=dst, in0=logs(piece)[:, first : first + n], in1=picked(i, lo, n), op=ALU.subtract)
-            nc.sync.dma_start(out=out[P * i : P * (i + 1), lo : lo + n], in_=dst)
+            result = sb(f"result_{piece}_{first}", [P, n], F32, tag)
+            engine.tensor_tensor(out=result[:], in0=logs(piece)[:, first : first + n], in1=picked(i, lo, n), op=ALU.subtract)
+            nc.sync.dma_start(out=out[P * i : P * (i + 1), lo : lo + n], in_=result[:])
 
         nc.sync.dma_start(offsets[:], offs)
+        tab_scale = sb("tab_scale", [P, T // 4], I32)
         nc.vector.memset(tab_scale[32:64, :], 0)
         nc.vector.memset(tab_scale[64:P, :], 0)
-        nc.vector.memset(seed[:, 0:ONES], 1.0)
+        one = sb("one", [P, ONES], F32)
+        nc.vector.memset(one[:], 1.0)
         for a in range(PASSES):
-            nc.vector.memset(v_scale[a][:].bitcast(I32), 0)
-        for name in ("zero00", "zero_ws", "sin1", "sin2", "sin3", "sin6", "sin7"):
-            nc.gpsimd.memset(held(name), 0.0)
-        nc.gpsimd.memset(held("early_log"), 1.0)
-        nc.scalar.activation(out=warm[:], in_=seed[:, 0:ONES], func=ACT.Ln)
+            nc.vector.memset(v_scale(a)[:].bitcast(I32), 0)
+        share_zero = sb("share_zero", [P, SMALL // 4], F32)[:, 0:ONES]
+        zero_bias = {
+            (SIN, 1): sq_scale(COS, 1)[:, QUARTER : QUARTER + 32].bitcast(F32),
+            (SIN, 3): picked(1, QUARTER, ONES),
+            (SIN, 6): picked(2, 0, ONES),
+            (SIN, 7): picked(2, QUARTER, ONES),
+        }
+        for zero in [share_zero] + list(zero_bias.values()):
+            nc.gpsimd.memset(zero, 0.0)
+        early_one = block_column(SIN, 5)
+        share_one = block_column(COS, 5)
+        for ones in (early_one, share_one):
+            nc.gpsimd.memset(ones, 1.0)
+        nc.scalar.activation(out=sb("warm", [P, ONES], F32)[:], in_=one[:], func=ACT.Ln)
 
         nc.sync.dma_start(out=tab_scale[0:32, :], in_=tab_scales.rearrange("a q t -> (a q) t").bitcast(I32))
         load_tab_words(0)
         load_w(COS, 0)
         load_w(COS, 1)
+        flat_picked = sb("flat_picked", [P, S], U8)
         nc.vector.tensor_copy(out=flat_picked[:], in_=tab_scale[:].bitcast(U8).indirect(list_slice(0, S)))
-        one = placed("one", [P, ONES], F32)
-        nc.vector.tensor_copy(out=one[:], in_=seed[:, 0:ONES])
-        wm_word = placed("wm_word", [P, 2 * N], U8)
-        wm_scale = placed("wm_scale", [P, N // 4], I32)
-        nc.gpsimd.memset(wm_scale[:], 0)
         moves = [(a, q) for a in range(PASSES) for q in range(QUADRANTS)]
         for a, q in moves[1:7]:
             move_scales(a, q)
         load_tab_words(1)
         move_scales(*moves[7])
         load_w(SIN, 0)
+
+        gather_words(0, 0, S)
         load_w(SIN, 1)
         load_floor(0)
+        wm_word = sb("wm_word", [P, 2 * N], U8)
+        wm_scale = sb("wm_scale", [P, N // 4], I32)
+        nc.gpsimd.memset(wm_scale[:], 0)
         nc.sync.dma_start(out=wm_word[:].bitcast(I32), in_=wm_words[0].bitcast(I32))
         for q in range(QUADRANTS):
             nc.sync.dma_start(out=wm_scale[32 * q : 32 * q + 4, :], in_=wm_scales[0, 4 * q : 4 * q + 4, :].bitcast(I32))
-        load_floor(1)
-        load_floor(2)
-
-        gather_words(0, 0, S)
         move_scales(*moves[0])
         round_w(COS, 0)
+        load_floor(1)
+        load_floor(2)
         round_w(COS, 1)
         quantise_w(COS, 0)
         open_first_products(COS)
@@ -314,46 +337,47 @@ def tile_list_voiced_log_spectra_kernel(tc, tab_words, tab_scales, offs, wc, ws,
             gather_words(1, lo, n)
         round_w(SIN, 0)
         quantise_w(SIN, 0)
-        first_products(COS, range(4))
+        first_products(COS, range(5))
         round_w(SIN, 1)
         quantise_squares(COS, 0, HALF)
         quantise_w(SIN, 1)
+        first_products(COS, range(5, 8))
+        quantise_squares(COS, HALF, QUARTER)
         gather_floor(0, 0, S)
-        first_products(COS, range(4, 8))
         open_first_products(SIN)
         first_products(SIN, range(5))
         quantise_squares(SIN, 0, QUARTER)
-        quantise_squares(COS, HALF, HALF)
+        quantise_squares(COS, HALF + QUARTER, QUARTER)
         gather_floor(1, 0, QUARTER)
         quantise_squares(SIN, QUARTER, QUARTER)
         gather_floor(1, QUARTER, S - QUARTER)
         first_pass(SIN, 5, 1)
         for f in (COS, SIN):
-            second_passes("a0", f)
+            second_passes("pair0", f)
         for b in range(6, 8):
             for a in range(PASSES):
                 first_pass(SIN, b, a)
-        logarithm("a0")
-        subtract_two_bands(nc.gpsimd, "a0")
+        logarithm("pair0")
+        subtract_pair("pair0")
         for b in range(5, 8):
             square(SIN, b)
         gather_floor(2, 0, QUARTER)
         quantise_squares(SIN, HALF, HALF)
         gather_floor(2, QUARTER, S - QUARTER)
 
-        for piece in ("a1", "c0"):
+        for piece in ("pair1", "early2"):
             for f in (COS, SIN):
                 second_passes(piece, f)
             logarithm(piece)
         for f in (COS, SIN):
-            for piece in ("b1", "b0", "b2"):
+            for piece in ("late1", "late0", "late2"):
                 second_passes(piece, f)
-        for piece in ("b1", "b0", "b2"):
+        for piece in ("late1", "late0", "late2"):
             logarithm(piece)
-        subtract_two_bands(nc.gpsimd, "a1")
-        subtract_band(nc.gpsimd, "c0", placed("result_c0_first", [P, QUARTER], F32), 0, QUARTER, 0)
-        subtract_band(nc.vector, "b1", placed("result_b1", [P, HALF], F32), 0, HALF, 0)
-        subtract_band(nc.vector, "c0", placed("result_c0_rest", [P, QUARTER], F32), QUARTER, QUARTER, 0)
-        subtract_band(nc.vector, "b0", placed("result_b0", [P, HALF], F32), 0, HALF, 0)
+        subtract_pair("pair1")
+        subtract_band(nc.gpsimd, "early2", 0, QUARTER)
+        subtract_band(nc.vector, "late1", 0, HALF)
+        subtract_band(nc.vector, "early2", QUARTER, QUARTER, tag="picked2_first")
+        subtract_band(nc.vector, "late0", 0, HALF)
         for first in (0, QUARTER):
-            subtract_band(nc.vector, "b2", placed("result_b2", [P, HALF], F32), first, QUARTER, first)
+            subtract_band(nc.vector, "late2", first, QUARTER)

@@ -38,11 +38,11 @@ SECOND_PASS_SLICES = ((0, BLOCK), (BLOCK, BLOCK), (QUARTER, QUARTER), (HALF, HAL
 
 PIECES = {
     "pair0": (0, 2, 0, QUARTER, (COS, 6)),
-    "pair1": (0, 2, QUARTER, QUARTER, (COS, 7)),
-    "early2": (2, 1, 0, HALF, (SIN, 0)),
-    "late1": (1, 1, HALF, HALF, (SIN, 1)),
-    "late0": (0, 1, HALF, HALF, (SIN, 2)),
-    "late2": (2, 1, HALF, HALF, (SIN, 5)),
+    "pair1": (0, 2, QUARTER, QUARTER, (COS, 6)),
+    "early2": (2, 1, 0, HALF, (SIN, 5)),
+    "late1": (1, 1, HALF, HALF, (SIN, 0)),
+    "late0": (0, 1, HALF, HALF, (SIN, 1)),
+    "late2": (2, 1, HALF, HALF, (SIN, 2)),
 }
 
 BIG = 8192
@@ -190,13 +190,14 @@ def tile_list_voiced_log_spectra_kernel(tc, tab_words, tab_scales, offs, wc, ws,
                 return b % AHEAD[COS]
             if b < AHEAD[SIN]:
                 return (AHEAD[COS] + b) % BANKS
-            return sum_bank(SIN, b - 3)
+            return sum_bank(COS, 7) if b == AHEAD[SIN] else sum_bank(SIN, 4)
 
         sums = {}
 
         def first_pass(f, b, a):
             frames = slice(BLOCK * b, BLOCK * (b + 1))
-            if a == 0:
+            opening = 1 if (f, b) == (SIN, AHEAD[SIN]) else 0
+            if a == opening:
                 sums[(f, b)] = psum.tile([P, PACK, BLOCK], F32, name="sums", tag=f"bank{sum_bank(f, b)}")
             for t in range(PACK):
                 w_cols = slice(P * t, P * (t + 1))
@@ -206,8 +207,8 @@ def tile_list_voiced_log_spectra_kernel(tc, tab_words, tab_scales, offs, wc, ws,
                     lhsT_scale=w_scale(f, a)[:, w_cols],
                     rhs=v_word(a)[:, frames].bitcast(FP8X4),
                     rhs_scale=v_scale(a)[4 * a : P, frames],
-                    start=(a == 0 and t == 0),
-                    stop=(a == PASSES - 1 and t == PACK - 1),
+                    start=(a == opening and t == 0),
+                    stop=(a != opening and t == PACK - 1),
                 )
 
         def square(f, b):
@@ -354,9 +355,10 @@ def tile_list_voiced_log_spectra_kernel(tc, tab_words, tab_scales, offs, wc, ws,
         first_pass(SIN, 5, 1)
         for f in (COS, SIN):
             second_passes("pair0", f)
-        for b in range(6, 8):
-            for a in range(PASSES):
-                first_pass(SIN, b, a)
+        for a in (1, 0):
+            first_pass(SIN, 6, a)
+        for a in (0, 1):
+            first_pass(SIN, 7, a)
         logarithm("pair0")
         subtract_pair("pair0")
         for b in range(5, 8):

from contextlib import ExitStack

import concourse.mybir as mybir

K, H, N, T, S = 1024, 512, 384, 2048, 1024
FLOPS = 2 * (2 * K * H * S + 2 * H * N * S)

F32 = mybir.dt.float32
BF16 = mybir.dt.bfloat16
I32 = mybir.dt.int32
U32 = mybir.dt.uint32
U16 = mybir.dt.uint16
U8 = mybir.dt.uint8
FP8X4 = mybir.dt.float8_e4m3fn_x4
FP4X4 = mybir.dt.float4_e2m1fn_x4
ACT = mybir.ActivationFunctionType
ALU = mybir.AluOpType

P = 128
PACK = 4
K_PASS = P * PACK
PASSES = K // K_PASS
COS, SIN = 0, 1
BLOCK = 128
HALF = 512
BLOCKS_PER_HALF = HALF // BLOCK
BAND_TILES = N // P
QUADRANTS = 4
LIST_ROWS = 16
ONES = 8

QUARTER = 256
BLOCKS = S // BLOCK
BANKS = 8
AHEAD = (4, 6)
SCALAR_SHARE = {(COS, 0): 72, (COS, 1): 56, (SIN, 0): 0, (SIN, 1): 40}
SECOND_PASS_SLICES = ((0, BLOCK), (BLOCK, BLOCK), (QUARTER, QUARTER), (HALF, HALF))

PIECES = {
    "pair0": (0, 2, 0, QUARTER, (COS, 6)),
    "pair1": (0, 2, QUARTER, QUARTER, (COS, 6)),
    "early2": (2, 1, 0, HALF, (SIN, 5)),
    "late1": (1, 1, HALF, HALF, (SIN, 0)),
    "late0": (0, 1, HALF, HALF, (SIN, 1)),
    "late2": (2, 1, HALF, HALF, (SIN, 2)),
}

BIG = 8192
GAP = 2048
SMALL = 128
FLOORS = 3 * BIG + GAP
BEHIND = FLOORS + BAND_TILES * BIG
PLACE = {
    "tab_word1": 0,
    "w_raw10": BIG,
    "w_raw11": 2 * BIG,
    "wm_scale": 3 * BIG,
    "wm_word": 3 * BIG + GAP // 2,
    "floor0": FLOORS,
    "floor1": FLOORS + BIG,
    "floor2": FLOORS + 2 * BIG,
    "tab_scale": BIG - GAP // 2,
    "tab_word0": 3 * BIG - BIG // 2,
    "w_raw00": FLOORS + 2 * BIG - BIG // 2,
    "w_raw01": BEHIND,
    "v_word1": BEHIND,
    "sq_scale00": BEHIND + BIG,
    "share_zero": BEHIND + BIG + HALF - SMALL // 2,
    "sq_bf_cos768": BEHIND + BIG + HALF,
}


def tile_list_voiced_log_spectra_kernel(tc, tab_words, tab_scales, offs, wc, ws, wm_words, wm_scales, gT, out):
    nc = tc.nc
    with ExitStack() as ctx:
        keep = ctx.enter_context(tc.tile_pool(name="keep", bufs=1))
        area = ctx.enter_context(tc.tile_pool(name="area", bufs=1))
        psum = ctx.enter_context(tc.psum_pool(name="psum", bufs=1))

        offsets = keep.tile([P, S // LIST_ROWS], U16, name="offsets")
        made = {}

        def sb(name, shape, dtype, tag=None):
            if name not in made and name in PLACE:
                made[name] = area.tile(shape, dtype, name=name, offset=PLACE[name], align_bytes=64)
            if name not in made:
                made[name] = keep.tile(shape, dtype, name=name, tag=tag or name, align_bytes=64)
            return made[name]

        def tab_word(a):
            return sb(f"tab_word{a}", [P, T], I32)

        def w_raw(f, a):
            return sb(f"w_raw{f}{a}", [P, PACK, H], F32)

        def floor(i):
            return sb(f"floor{i}", [P, T], F32)

        def w_bf(f, a):
            tag = "w_bf01" if (f, a) == (SIN, 0) else None
            return sb(f"w_bf{f}{a}", [P, PACK, P, PACK], BF16, tag)

        def w_word(f, a):
            return sb(f"w_word{f}{a}", [P, H], U32)

        def w_scale(f, a):
            return sb(f"w_scale{f}{a}", [P, H], U8)

        def v_word(a):
            return sb(f"v_word{a}", [P, S], U32)

        def v_scale(a):
            return sb(f"v_scale{a}", [P, S], U8)

        def sq_bf(f, lo, n):
            if f == COS and lo >= HALF:
                first = lo - lo % QUARTER
                return sb(f"sq_bf_cos{first}", [P, QUARTER, PACK], BF16)[:, lo - first : lo - first + n, :]
            first = lo - lo % HALF
            return sb(f"sq_bf{f}{first // HALF}", [P, HALF, PACK], BF16)[:, lo - first : lo - first + n, :]

        def block_column(f, b):
            return sq_bf(f, BLOCK * b, BLOCK).rearrange("p j t -> p (j t)").bitcast(F32)[:, 0:ONES]

        def sq_word(f, h):
            return sb(f"sq_word{f}{h}", [P, HALF], U32)

        def sq_scale(f, h):
            return sb(f"sq_scale{f}{h}", [P, HALF], U8)

        def picked_pair(lo, n):
            return sb("picked01", [P, 2, S], F32)[:, :, lo : lo + n]

        def picked(i, lo, n):
            if i < 2:
                return picked_pair(lo, n)[:, i, :]
            if lo < QUARTER:
                return sb("picked2_first", [P, QUARTER], F32)[:, lo : lo + n]
            return sb("picked2_rest", [P, S - QUARTER], F32)[:, lo - QUARTER : lo - QUARTER + n]

        def logs(piece):
            return sb(f"logs_{piece}", [P, HALF], F32)

        def load_tab_words(a):
            nc.sync.dma_start(out=tab_word(a)[:], in_=tab_words[a].rearrange("p t i -> p (t i)").bitcast(I32))

        def load_w(f, a):
            rows = (wc, ws)[f][K_PASS * a : K_PASS * (a + 1), :]
            nc.sync.dma_start(out=w_raw(f, a)[:], in_=rows.rearrange("(p j) c -> p j c", j=PACK))

        def load_floor(i):
            nc.sync.dma_start(out=floor(i)[:], in_=gT[P * i : P * (i + 1), :])

        def move_scales(a, q):
            src = flat_picked[16 * a + 4 * q : 16 * a + 4 * q + 4, :].bitcast(I32)
            dst = v_scale(a)[32 * q + 4 * a : 32 * q + 4 * a + 4, :].bitcast(I32)
            if (a, q) == (0, 0):
                nc.vector.tensor_copy(out=dst, in_=src)
            else:
                nc.sync.dma_start(out=dst, in_=src)

        def list_slice(lo, n):
            return offsets[:, lo // LIST_ROWS : (lo + n) // LIST_ROWS]

        def gather_words(a, lo, n):
            nc.vector.tensor_copy(out=v_word(a)[:, lo : lo + n], in_=tab_word(a)[:].bitcast(U32).indirect(list_slice(lo, n)))

        def gather_floor(i, lo, n):
            nc.vector.tensor_copy(out=picked(i, lo, n), in_=floor(i)[:].indirect(list_slice(lo, n)))

        def round_w(f, a):
            src = w_raw(f, a)[:].rearrange("p j (m t) -> p m j t", t=PACK)
            dst = w_bf(f, a)[:].rearrange("p t m j -> p m j t")
            cut = SCALAR_SHARE[(f, a)]
            if (f, a) == (SIN, 1):
                nc.scalar.activation(out=dst[:, 0:cut], in_=src[:, 0:cut], func=ACT.Identity, bias=share_zero[:, 0:1], scale=share_one[:, 0:1])
            elif cut > 0:
                nc.scalar.activation(out=dst[:, 0:cut], in_=src[:, 0:cut], func=ACT.Copy)
            nc.vector.tensor_copy(out=dst[:, cut:P], in_=src[:, cut:P])

        def quantise_w(f, a):
            nc.vector.quantize_mx(
                out=w_word(f, a)[:].bitcast(FP8X4),
                scales=w_scale(f, a)[:],
                in_=w_bf(f, a)[:].rearrange("p t m j -> p (t m j)"),
            )

        def sum_bank(f, b):
            if f == COS:
                return b % AHEAD[COS]
            if b < AHEAD[SIN]:
                return (AHEAD[COS] + b) % BANKS
            return sum_bank(COS, 7) if b == AHEAD[SIN] else sum_bank(SIN, 4)

        sums = {}

        def first_pass(f, b, a):
            frames = slice(BLOCK * b, BLOCK * (b + 1))
            opening = 1 if (f, b) == (SIN, AHEAD[SIN]) else 0
            if a == opening:
                sums[(f, b)] = psum.tile([P, PACK, BLOCK], F32, name="sums", tag=f"bank{sum_bank(f, b)}")
            for t in range(PACK):
                w_cols = slice(P * t, P * (t + 1))
                nc.tensor.matmul_mx(
                    out=sums[(f, b)][:, t, :],
                    lhsT=w_word(f, a)[:, w_cols].bitcast(FP8X4),
                    lhsT_scale=w_scale(f, a)[:, w_cols],
                    rhs=v_word(a)[:, frames].bitcast(FP8X4),
                    rhs_scale=v_scale(a)[4 * a : P, frames],
                    start=(a == opening and t == 0),
                    stop=(a != opening and t == PACK - 1),
                )

        def square(f, b):
            zero = zero_bias.get((f, b))
            nc.scalar.activation(
                out=sq_bf(f, BLOCK * b, BLOCK),
                in_=sums[(f, b)][:].rearrange("p t j -> p j t"),
                func=ACT.Square,
                bias=0.0 if zero is None else zero[:, 0:1],
            )

        def open_first_products(f):
            for b in range(AHEAD[f]):
                first_pass(f, b, 0)

        def first_products(f, blocks):
            for b in blocks:
                first_pass(f, b, 1)
                square(f, b)
                if f == COS and b + AHEAD[f] < BLOCKS:
                    first_pass(f, b + AHEAD[f], 0)

        def quantise_squares(f, lo, n):
            h, first = divmod(lo, HALF)
            cols = slice(first, first + n)
            nc.vector.quantize_mx(
                out=sq_word(f, h)[:, cols].bitcast(FP8X4),
                scales=sq_scale(f, h)[:, cols],
                in_=sq_bf(f, lo, n).rearrange("p j t -> p (j t)"),
            )

        power = {}

        def second_passes(piece, f):
            first_band, bands, lo, n, follows = PIECES[piece]
            h, first = divmod(lo, HALF)
            cols = slice(first, first + n)
            if f == COS:
                power[piece] = psum.tile([P, HALF], F32, name="power", tag=f"bank{sum_bank(*follows)}")
            for k in range(bands):
                i = first_band + k
                nc.tensor.matmul_mx(
                    out=power[piece][:, n * k : n * (k + 1)],
                    lhsT=wm_word[:, 2 * P * i : 2 * P * (i + 1)].bitcast(FP4X4),
                    lhsT_scale=wm_scale[:].bitcast(U8)[:, P * i : P * (i + 1)],
                    rhs=sq_word(f, h)[:, cols].bitcast(FP8X4),
                    rhs_scale=sq_scale(f, h)[:, cols],
                    start=(f == COS and k == 0),
                    stop=(f == SIN and k == bands - 1),
                )

        def logarithm(piece):
            ones = early_one if piece == "pair0" else one
            nc.scalar.activation(out=logs(piece)[:], in_=power[piece][:], func=ACT.Ln, bias=ones[:, 0:1])

        def subtract_pair(piece):
            lo = PIECES[piece][2]
            result = sb(f"result_{piece}", [P, 2, QUARTER], F32)
            nc.gpsimd.tensor_tensor(
                out=result[:],
                in0=logs(piece)[:].rearrange("p (i j) -> p i j", i=2),
                in1=picked_pair(lo, QUARTER),
                op=ALU.subtract,
            )
            nc.sync.dma_start(out=out[0 : 2 * P, lo : lo + QUARTER].rearrange("(i p) j -> p i j", p=P), in_=result[:])

        def subtract_band(engine, piece, first, n, tag=None):
            i, lo = PIECES[piece][0], PIECES[piece][2] + first
            result = sb(f"result_{piece}_{first}", [P, n], F32, tag)
            engine.tensor_tensor(out=result[:], in0=logs(piece)[:, first : first + n], in1=picked(i, lo, n), op=ALU.subtract)
            nc.sync.dma_start(out=out[P * i : P * (i + 1), lo : lo + n], in_=result[:])

        nc.sync.dma_start(offsets[:], offs)
        tab_scale = sb("tab_scale", [P, T // 4], I32)
        nc.vector.memset(tab_scale[32:64, :], 0)
        nc.vector.memset(tab_scale[64:P, :], 0)
        one = sb("one", [P, ONES], F32)
        nc.vector.memset(one[:], 1.0)
        for a in range(PASSES):
            nc.vector.memset(v_scale(a)[:].bitcast(I32), 0)
        share_zero = sb("share_zero", [P, SMALL // 4], F32)[:, 0:ONES]
        zero_bias = {
            (SIN, 1): sq_scale(COS, 1)[:, QUARTER : QUARTER + 32].bitcast(F32),
            (SIN, 3): picked(1, QUARTER, ONES),
            (SIN, 6): picked(2, 0, ONES),
            (SIN, 7): picked(2, QUARTER, ONES),
        }
        for zero in [share_zero] + list(zero_bias.values()):
            nc.gpsimd.memset(zero, 0.0)
        early_one = block_column(SIN, 5)
        share_one = block_column(COS, 5)
        for ones in (early_one, share_one):
            nc.gpsimd.memset(ones, 1.0)
        nc.scalar.activation(out=sb("warm", [P, ONES], F32)[:], in_=one[:], func=ACT.Ln)

        nc.sync.dma_start(out=tab_scale[0:32, :], in_=tab_scales.rearrange("a q t -> (a q) t").bitcast(I32))
        load_tab_words(0)
        load_w(COS, 0)
        load_w(COS, 1)
        flat_picked = sb("flat_picked", [P, S], U8)
        nc.vector.tensor_copy(out=flat_picked[:], in_=tab_scale[:].bitcast(U8).indirect(list_slice(0, S)))
        moves = [(a, q) for a in range(PASSES) for q in range(QUADRANTS)]
        for a, q in moves[1:7]:
            move_scales(a, q)
        load_tab_words(1)
        move_scales(*moves[7])
        load_w(SIN, 0)

        gather_words(0, 0, S)
        load_w(SIN, 1)
        load_floor(0)
        wm_word = sb("wm_word", [P, 2 * N], U8)
        wm_scale = sb("wm_scale", [P, N // 4], I32)
        nc.gpsimd.memset(wm_scale[:], 0)
        nc.sync.dma_start(out=wm_word[:].bitcast(I32), in_=wm_words[0].bitcast(I32))
        for q in range(QUADRANTS):
            nc.sync.dma_start(out=wm_scale[32 * q : 32 * q + 4, :], in_=wm_scales[0, 4 * q : 4 * q + 4, :].bitcast(I32))
        move_scales(*moves[0])
        round_w(COS, 0)
        load_floor(1)
        load_floor(2)
        round_w(COS, 1)
        quantise_w(COS, 0)
        open_first_products(COS)
        quantise_w(COS, 1)
        for lo, n in SECOND_PASS_SLICES:
            gather_words(1, lo, n)
        round_w(SIN, 0)
        quantise_w(SIN, 0)
        first_products(COS, range(5))
        round_w(SIN, 1)
        quantise_squares(COS, 0, HALF)
        quantise_w(SIN, 1)
        first_products(COS, range(5, 8))
        quantise_squares(COS, HALF, QUARTER)
        gather_floor(0, 0, S)
        open_first_products(SIN)
        first_products(SIN, range(5))
        quantise_squares(SIN, 0, QUARTER)
        quantise_squares(COS, HALF + QUARTER, QUARTER)
        gather_floor(1, 0, QUARTER)
        quantise_squares(SIN, QUARTER, QUARTER)
        gather_floor(1, QUARTER, S - QUARTER)
        first_pass(SIN, 5, 1)
        for f in (COS, SIN):
            second_passes("pair0", f)
        for a in (1, 0):
            first_pass(SIN, 6, a)
        for a in (0, 1):
            first_pass(SIN, 7, a)
        logarithm("pair0")
        subtract_pair("pair0")
        for b in range(5, 8):
            square(SIN, b)
        gather_floor(2, 0, QUARTER)
        quantise_squares(SIN, HALF, HALF)
        gather_floor(2, QUARTER, S - QUARTER)

        for piece in ("pair1", "early2"):
            for f in (COS, SIN):
                second_passes(piece, f)
            logarithm(piece)
        for f in (COS, SIN):
            for piece in ("late1", "late0", "late2"):
                second_passes(piece, f)
        for piece in ("late1", "late0", "late2"):
            logarithm(piece)
        subtract_pair("pair1")
        subtract_band(nc.gpsimd, "early2", 0, QUARTER)
        subtract_band(nc.vector, "late1", 0, HALF)
        subtract_band(nc.vector, "early2", QUARTER, QUARTER, tag="picked2_first")
        subtract_band(nc.vector, "late0", 0, HALF)
        for first in (0, QUARTER):
            subtract_band(nc.vector, "late2", first, QUARTER)
